import numpy as np
import ml_dtypes


def mxq(x, axis, fmt="e4m3"):
    dtype, down = {"e4m3": (ml_dtypes.float8_e4m3fn, 7), "e5m2": (ml_dtypes.float8_e5m2, 14)}[fmt]
    v = np.moveaxis(np.asarray(x, np.float32).astype(ml_dtypes.bfloat16).astype(np.float64), axis, -1)
    blocks = v.reshape(v.shape[:-1] + (-1, 32))
    amax = np.abs(blocks).max(-1, keepdims=True)
    byte = np.maximum(np.where(amax > 0, np.frexp(amax)[1] - 1 + 127, 0) - down, 1)
    scale = np.exp2(byte - 127.0)
    codes = (blocks / scale).astype(np.float32).astype(dtype).astype(np.float64)
    return np.moveaxis((codes * scale).reshape(v.shape), -1, axis)


WIDE = False


def mx_kscale(k):
    if not WIDE:
        return np.ones(k)
    levels = np.array([10, -10, 5, -5, 0])
    if k % 512:
        return np.exp2(np.random.permutation(np.resize(levels, k // 32))).repeat(32)
    a = np.empty((k // 512, 16))
    for p in range(k // 512):
        a[p, :8] = np.random.permutation(np.resize(levels, 8))
        for g in range(8):
            far = levels[np.abs(levels - a[p, g]) >= 10]
            a[p, g + 8] = far[np.random.randint(len(far))]
    return np.exp2(a.ravel()).repeat(32)


def f64(x):
    return np.asarray(x).astype(np.float64)


def striped(idx):
    return np.tile(idx.reshape(-1, 16).T, (8, 1)).astype(np.uint16)


def unstriped(offs):
    return offs[:16].T.reshape(-1).astype(np.int64)


def striped8(idx):
    return np.concatenate([x.reshape(-1, 16).T for x in idx]).astype(np.uint16)


def runs(offs, k):
    lists = np.stack([offs[16 * r : 16 * r + 16].T.reshape(-1) for r in range(8)]).astype(np.int64)
    return lists[np.arange(k) % 512 // 64]


def pack_weight(w):
    k, n = w.shape
    w = f64(np.asarray(w, np.float32).astype(ml_dtypes.bfloat16)).reshape(k // 32, 32, n)
    amax = np.abs(w).max(1)
    byte = np.clip(np.where(amax > 0, np.frexp(amax)[1] - 1 + 127 - 7, 1), 1, 254)
    scaled = (w * np.exp2(127.0 - byte)[:, None, :]).reshape(k, n).astype(np.float32)
    words = np.ascontiguousarray(scaled.reshape(k // 512, 128, 4, n).transpose(0, 1, 3, 2)).astype(ml_dtypes.float8_e4m3fn).view(np.uint8)
    return words, np.ascontiguousarray(byte.astype(np.uint8).reshape(k // 512, 16, n))


def unpack_weight(words, scales):
    g, p, n, _ = words.shape
    vals = np.ascontiguousarray(words).view(ml_dtypes.float8_e4m3fn).astype(np.float64) * np.repeat(np.exp2(scales.astype(np.float64) - 127.0), 8, axis=1)[..., None]
    return vals.transpose(0, 1, 3, 2).reshape(g * 512, n)

def planes(y):
    n, m = y.shape
    v = y.astype(np.float32).astype(ml_dtypes.bfloat16).astype(np.float64).reshape(n // 32, 32, m)
    top = np.abs(v).max(1)
    byte = np.clip(np.where(top > 0, np.frexp(top)[1] - 1 + 127 - 7, 1), 1, 254)
    codes = (v * np.exp2(127.0 - byte)[:, None, :]).reshape(n, m).astype(np.float32).astype(ml_dtypes.float8_e4m3fn).view(np.uint8)
    words = codes.reshape(n // 512, 128, 4, m).transpose(0, 1, 3, 2)
    return np.ascontiguousarray(words), np.ascontiguousarray(byte.astype(np.uint8).reshape(n // 512, 16, m))


K, T, S, N, U = 512, 2048, 512, 512, 2048


def setup_inputs():
    n = np.random.standard_normal
    s = mx_kscale(K)[:, None]
    packed_xT = pack_weight(n((K, T)) * s)
    return {
        "x_words": packed_xT[0],
        "x_scales": packed_xT[1],
        "mem": n((N, U)).astype(np.float32),
        "w1": (n((K, N)) / np.sqrt(K) / s).astype(np.float32),
        "offs": striped8(np.stack([np.random.permutation(T)[:S] for _ in range(8)])),
        "slot": striped(np.random.permutation(U)[:S]),
    }


def reference(x_words, x_scales, mem, w1, offs, slot):
    xq = unpack_weight(x_words, x_scales)[np.arange(K)[:, None], runs(offs, K)]
    y = mxq(f64(w1), 0, "e4m3").T @ xq
    out = f64(mem).copy()
    out[:, unstriped(slot)] = y
    return (out,) + planes(out)

@@ -1,0 +1,141 @@
+from contextlib import ExitStack
+
+import concourse.mybir as mybir
+
+K, T, S, N, U = 512, 2048, 512, 512, 2048
+FLOPS = 2 * K * N * S
+
+F32 = mybir.dt.float32
+BF16 = mybir.dt.bfloat16
+I32 = mybir.dt.int32
+U32 = mybir.dt.uint32
+U16 = mybir.dt.uint16
+U8 = mybir.dt.uint8
+FP8X4 = mybir.dt.float8_e4m3fn_x4
+
+P = 128
+PACK = 4
+CHUNKS = (256, 512, 512, 256, 256, 256)
+SCALAR_FROM = 4
+STORE_AFTER = {1: 0, 2: 2, 4: 3, 5: 5}
+
+
+def tile_picked_phput_none_po_kernel(tc, x_words, x_scales, mem, w1, offs, slot, out_0, out_1, out_2):
+    nc = tc.nc
+    with ExitStack() as ctx:
+        lists = ctx.enter_context(tc.tile_pool(name="lists", bufs=1))
+        keep = ctx.enter_context(tc.tile_pool(name="keep", bufs=1))
+        psum = ctx.enter_context(tc.psum_pool(name="psum", bufs=1))
+
+        offs_sb = lists.tile([P, S // 16], U16, name="offs_sb")
+        slot_sb = lists.tile([P, S // 16], U16, name="slot_sb")
+        scale_table = keep.tile([P, T], U8, name="scale_table", align_bytes=64)
+        x_scale = keep.tile([P, S], U8, name="x_scale", align_bytes=64)
+        nc.vector.memset(scale_table[:].bitcast(I32), 0)
+        nc.vector.memset(x_scale[:].bitcast(I32), 0)
+
+        nc.sync.dma_start(offs_sb[:], offs)
+        scale_rows = x_scales[0].rearrange("(r e) c -> e r c", e=2)
+        w_raw = keep.tile([P, PACK, N], F32, name="w_raw", tag="slot_a", align_bytes=64)
+        w_rows = w1.rearrange("(p j) n -> p j n", j=PACK)
+        nc.sync.dma_start(w_raw[:, 0:1, :], w_rows[:, 0:1, :])
+        for e in range(2):
+            nc.sync.dma_start(scale_table[e:P:16, :].bitcast(I32), scale_rows[e].bitcast(I32))
+        nc.sync.dma_start(w_raw[:, 1:4, :], w_rows[:, 1:4, :])
+        word_table = keep.tile([P, T], U32, name="word_table", tag="slot_b", align_bytes=64)
+        nc.sync.dma_start(word_table[:].bitcast(I32), x_words[0].rearrange("p c r -> p (c r)").bitcast(I32))
+
+        mem_rows = mem.rearrange("(p t) c -> t p c", t=PACK)
+        out_rows = out_0.rearrange("(p t) c -> t p c", t=PACK)
+        windows = []
+        for t in range(2):
+            window = keep.tile([P, U], F32, name="window%d" % t, align_bytes=64)
+            nc.sync.dma_start(window[:], mem_rows[t])
+            windows.append(window)
+            if t == 0:
+                nc.sync.dma_start(slot_sb[:], slot)
+
+        picked_scale = keep.tile([P, S], U8, name="picked_scale", align_bytes=64)
+        nc.vector.tensor_copy(picked_scale[:], scale_table[:].indirect(offs_sb[:]))
+        for e in range(2):
+            nc.scalar.dma_start(x_scale[2 + e : P : 32, :].bitcast(I32), picked_scale[16 + e : P : 32, :].bitcast(I32))
+        for q in range(4):
+            nc.vector.tensor_copy(x_scale[32 * q : 32 * q + 2, :].bitcast(I32), picked_scale[32 * q : 32 * q + 2, :].bitcast(I32))
+
+        w_bf = keep.tile([P, PACK * N], BF16, name="w_bf", align_bytes=64)
+        nc.vector.tensor_copy(
+            w_bf[:].rearrange("p (t m j) -> p m j t", t=PACK, j=PACK),
+            w_raw[:].rearrange("p j (m t) -> p m j t", t=PACK),
+        )
+        w_codes = keep.tile([P, N], U32, name="w_codes", align_bytes=64)
+        w_scale = keep.tile([P, N], U8, name="w_scale", align_bytes=64)
+        nc.vector.quantize_mx(out=w_codes[:].bitcast(FP8X4), scales=w_scale[:], in_=w_bf[:])
+
+        x_codes = keep.tile([P, S], U32, name="x_codes", align_bytes=64)
+        nc.vector.tensor_copy(x_codes[:], word_table[:].indirect(offs_sb[:]))
+
+        for t, tag in ((2, "slot_a"), (3, "slot_b")):
+            window = keep.tile([P, U], F32, name="window%d" % t, tag=tag, align_bytes=64)
+            nc.sync.dma_start(window[:], mem_rows[t])
+            windows.append(window)
+
+        ys = []
+        for t in range(PACK):
+            acc = psum.tile([P, S], F32, name="acc%d" % t)
+            cols = slice(t * P, (t + 1) * P)
+            nc.tensor.matmul_mx(
+                out=acc[:],
+                lhsT=w_codes[:, cols].bitcast(FP8X4),
+                lhsT_scale=w_scale[:, cols],
+                rhs=x_codes[:].bitcast(FP8X4),
+                rhs_scale=x_scale[:],
+                start=True,
+                stop=True,
+            )
+            y = keep.tile([P, S], F32, name="y%d" % t)
+            nc.scalar.copy(y[:], acc[:])
+            ys.append(y)
+
+        starts = [sum(CHUNKS[:i]) for i in range(len(CHUNKS) + 1)]
+        pairs = keep.tile([P, PACK * U], BF16, name="pairs", align_bytes=64)
+        halves = pairs[:].rearrange("p (h c e) -> p h c e", h=2, e=2)
+        for t in range(PACK):
+            nc.vector.tensor_copy(windows[t][:].indirect(slot_sb[:]), ys[t][:])
+            nc.sync.dma_start(out_rows[t], windows[t][:])
+            if t < 2:
+                nc.scalar.copy(halves[:, 0, :, t], windows[t][:])
+            else:
+                nc.vector.tensor_copy(halves[:, 1, 0 : starts[1], t - 2], windows[t][:, 0 : starts[1]])
+                edges = [starts[1], U] if t == 2 else starts[1:SCALAR_FROM + 1] + [U]
+                for lo, hi in zip(edges[:-1], edges[1:]):
+                    nc.scalar.copy(halves[:, 1, lo:hi, t - 2], windows[t][:, lo:hi])
+
+        out_scale = keep.tile([P, U], U8, name="out_scale", align_bytes=64)
+        codes = keep.tile([P, U], U32, name="codes", align_bytes=64)
+        out_words = out_1[0].rearrange("p c r -> p (c r)").bitcast(I32)
+        grouped = [keep.tile([P, PACK * n], BF16, name="grouped%d" % i, align_bytes=64) for i, n in enumerate(CHUNKS)]
+
+        def weave(i):
+            word = U32 if i >= SCALAR_FROM else I32
+            dst = grouped[i][:].bitcast(word).rearrange("p (c h) -> p c h", h=2)
+            src = pairs[:].bitcast(word).rearrange("p (h c) -> p c h", h=2)[:, starts[i] : starts[i + 1], :]
+            if i >= SCALAR_FROM:
+                nc.scalar.copy(dst, src)
+            else:
+                nc.vector.tensor_copy(dst, src)
+
+        def quantise(i):
+            cols = slice(starts[i], starts[i + 1])
+            nc.vector.quantize_mx(out=codes[:, cols].bitcast(FP8X4), scales=out_scale[:, cols], in_=grouped[i][:])
+            if i in STORE_AFTER:
+                stored = slice(starts[STORE_AFTER[i]], starts[i + 1])
+                nc.sync.dma_start(out_words[:, stored], codes[:, stored].bitcast(I32))
+
+        weave(0)
+        for i in range(1, len(CHUNKS)):
+            weave(i)
+            quantise(i - 1)
+        quantise(len(CHUNKS) - 1)
+        for q in range(4):
+            queue = nc.scalar if q % 2 else nc.sync
+            queue.dma_start(out_2[0, 4 * q : 4 * q + 4, :].bitcast(I32), out_scale[32 * q : 32 * q + 4, :].bitcast(I32))

@@ -15,9 +15,10 @@ FP8X4 = mybir.dt.float8_e4m3fn_x4
 
 P = 128
 PACK = 4
-CHUNKS = (256, 512, 512, 256, 256, 256)
+GROUP = 512
+CHUNKS = ((0, 256), (512, 1024), (1024, 1536), (256, 512), (1536, 1792), (1792, 2048))
 SCALAR_FROM = 4
-STORE_AFTER = {1: 0, 2: 2, 4: 3, 5: 5}
+STORE_AFTER = {2: (512, 1536), 3: (0, 512), 4: (1536, 1792), 5: (1792, 2048)}
 
 
 def tile_picked_phput_none_po_kernel(tc, x_words, x_scales, mem, w1, offs, slot, out_0, out_1, out_2):
@@ -29,44 +30,34 @@ def tile_picked_phput_none_po_kernel(tc, x_words, x_scales, mem, w1, offs, slot,
 
         offs_sb = lists.tile([P, S // 16], U16, name="offs_sb")
         slot_sb = lists.tile([P, S // 16], U16, name="slot_sb")
-        scale_table = keep.tile([P, T], U8, name="scale_table", align_bytes=64)
+        scale_table = keep.tile([P, T], U8, name="scale_table", tag="slot0", align_bytes=64)
         x_scale = keep.tile([P, S], U8, name="x_scale", align_bytes=64)
         nc.vector.memset(scale_table[:].bitcast(I32), 0)
         nc.vector.memset(x_scale[:].bitcast(I32), 0)
 
         nc.sync.dma_start(offs_sb[:], offs)
         scale_rows = x_scales[0].rearrange("(r e) c -> e r c", e=2)
-        w_raw = keep.tile([P, PACK, N], F32, name="w_raw", tag="slot_a", align_bytes=64)
+        w_raw = [keep.tile([P, PACK, N // 2], F32, name="w_raw%d" % h, tag="slot%d" % (h + 1), align_bytes=64) for h in range(2)]
         w_rows = w1.rearrange("(p j) n -> p j n", j=PACK)
-        nc.sync.dma_start(w_raw[:, 0:1, :], w_rows[:, 0:1, :])
+        nc.sync.dma_start(w_raw[0][:], w_rows[:, :, 0 : N // 2])
         for e in range(2):
             nc.sync.dma_start(scale_table[e:P:16, :].bitcast(I32), scale_rows[e].bitcast(I32))
-        nc.sync.dma_start(w_raw[:, 1:4, :], w_rows[:, 1:4, :])
-        word_table = keep.tile([P, T], U32, name="word_table", tag="slot_b", align_bytes=64)
+        nc.sync.dma_start(w_raw[1][:], w_rows[:, :, N // 2 : N])
+        word_table = keep.tile([P, T], U32, name="word_table", tag="slot3", align_bytes=64)
         nc.sync.dma_start(word_table[:].bitcast(I32), x_words[0].rearrange("p c r -> p (c r)").bitcast(I32))
-
-        mem_rows = mem.rearrange("(p t) c -> t p c", t=PACK)
-        out_rows = out_0.rearrange("(p t) c -> t p c", t=PACK)
-        windows = []
-        for t in range(2):
-            window = keep.tile([P, U], F32, name="window%d" % t, align_bytes=64)
-            nc.sync.dma_start(window[:], mem_rows[t])
-            windows.append(window)
-            if t == 0:
-                nc.sync.dma_start(slot_sb[:], slot)
+        nc.sync.dma_start(slot_sb[:], slot)
 
         picked_scale = keep.tile([P, S], U8, name="picked_scale", align_bytes=64)
         nc.vector.tensor_copy(picked_scale[:], scale_table[:].indirect(offs_sb[:]))
         for e in range(2):
-            nc.scalar.dma_start(x_scale[2 + e : P : 32, :].bitcast(I32), picked_scale[16 + e : P : 32, :].bitcast(I32))
+            nc.sync.dma_start(x_scale[2 + e : P : 32, :].bitcast(I32), picked_scale[16 + e : P : 32, :].bitcast(I32))
         for q in range(4):
             nc.vector.tensor_copy(x_scale[32 * q : 32 * q + 2, :].bitcast(I32), picked_scale[32 * q : 32 * q + 2, :].bitcast(I32))
 
         w_bf = keep.tile([P, PACK * N], BF16, name="w_bf", align_bytes=64)
-        nc.vector.tensor_copy(
-            w_bf[:].rearrange("p (t m j) -> p m j t", t=PACK, j=PACK),
-            w_raw[:].rearrange("p j (m t) -> p m j t", t=PACK),
-        )
+        w_dealt = w_bf[:].rearrange("p (t h m j) -> p h m j t", t=PACK, h=2, j=PACK)
+        for h in range(2):
+            nc.vector.tensor_copy(w_dealt[:, h], w_raw[h][:].rearrange("p j (m t) -> p m j t", t=PACK))
         w_codes = keep.tile([P, N], U32, name="w_codes", align_bytes=64)
         w_scale = keep.tile([P, N], U8, name="w_scale", align_bytes=64)
         nc.vector.quantize_mx(out=w_codes[:].bitcast(FP8X4), scales=w_scale[:], in_=w_bf[:])
@@ -74,8 +65,11 @@ def tile_picked_phput_none_po_kernel(tc, x_words, x_scales, mem, w1, offs, slot,
         x_codes = keep.tile([P, S], U32, name="x_codes", align_bytes=64)
         nc.vector.tensor_copy(x_codes[:], word_table[:].indirect(offs_sb[:]))
 
-        for t, tag in ((2, "slot_a"), (3, "slot_b")):
-            window = keep.tile([P, U], F32, name="window%d" % t, tag=tag, align_bytes=64)
+        mem_rows = mem.rearrange("(p t) c -> t p c", t=PACK)
+        out_rows = out_0.rearrange("(p t) c -> t p c", t=PACK)
+        windows = []
+        for t in range(PACK):
+            window = keep.tile([P, U], F32, name="window%d" % t, tag="slot%d" % t, align_bytes=64)
             nc.sync.dma_start(window[:], mem_rows[t])
             windows.append(window)
 
@@ -96,39 +90,42 @@ def tile_picked_phput_none_po_kernel(tc, x_words, x_scales, mem, w1, offs, slot,
             nc.scalar.copy(y[:], acc[:])
             ys.append(y)
 
-        starts = [sum(CHUNKS[:i]) for i in range(len(CHUNKS) + 1)]
-        pairs = keep.tile([P, PACK * U], BF16, name="pairs", align_bytes=64)
-        halves = pairs[:].rearrange("p (h c e) -> p h c e", h=2, e=2)
+        pairs = [keep.tile([P, PACK * (hi - lo)], BF16, name="pairs%d" % i, align_bytes=64) for i, (lo, hi) in enumerate(CHUNKS)]
         for t in range(PACK):
             nc.vector.tensor_copy(windows[t][:].indirect(slot_sb[:]), ys[t][:])
             nc.sync.dma_start(out_rows[t], windows[t][:])
-            if t < 2:
-                nc.scalar.copy(halves[:, 0, :, t], windows[t][:])
-            else:
-                nc.vector.tensor_copy(halves[:, 1, 0 : starts[1], t - 2], windows[t][:, 0 : starts[1]])
-                edges = [starts[1], U] if t == 2 else starts[1:SCALAR_FROM + 1] + [U]
-                for lo, hi in zip(edges[:-1], edges[1:]):
-                    nc.scalar.copy(halves[:, 1, lo:hi, t - 2], windows[t][:, lo:hi])
+            for i, (lo, hi) in enumerate(CHUNKS):
+                dst = pairs[i][:].rearrange("p (h c e) -> p h c e", h=2, e=2)[:, t // 2, :, t % 2]
+                src = windows[t][:, lo:hi]
+                if t >= 2 and i == 0:
+                    nc.vector.tensor_copy(dst, src)
+                else:
+                    nc.scalar.copy(dst, src)
 
-        out_scale = keep.tile([P, U], U8, name="out_scale", align_bytes=64)
+        out_scale = keep.tile([P, GROUP], U8, name="out_scale", align_bytes=64)
         codes = keep.tile([P, U], U32, name="codes", align_bytes=64)
         out_words = out_1[0].rearrange("p c r -> p (c r)").bitcast(I32)
-        grouped = [keep.tile([P, PACK * n], BF16, name="grouped%d" % i, align_bytes=64) for i, n in enumerate(CHUNKS)]
+        grouped = [keep.tile([P, PACK * (hi - lo)], BF16, name="grouped%d" % i, align_bytes=64) for i, (lo, hi) in enumerate(CHUNKS)]
 
         def weave(i):
             word = U32 if i >= SCALAR_FROM else I32
             dst = grouped[i][:].bitcast(word).rearrange("p (c h) -> p c h", h=2)
-            src = pairs[:].bitcast(word).rearrange("p (h c) -> p c h", h=2)[:, starts[i] : starts[i + 1], :]
+            src = pairs[i][:].bitcast(word).rearrange("p (h c) -> p c h", h=2)
             if i >= SCALAR_FROM:
                 nc.scalar.copy(dst, src)
             else:
                 nc.vector.tensor_copy(dst, src)
 
         def quantise(i):
-            cols = slice(starts[i], starts[i + 1])
-            nc.vector.quantize_mx(out=codes[:, cols].bitcast(FP8X4), scales=out_scale[:, cols], in_=grouped[i][:])
+            lo, hi = CHUNKS[i]
+            g = lo // GROUP
+            nc.vector.quantize_mx(
+                out=codes[:, lo:hi].bitcast(FP8X4),
+                scales=out_scale[4 * g : P, lo - g * GROUP : hi - g * GROUP],
+                in_=grouped[i][:],
+            )
             if i in STORE_AFTER:
-                stored = slice(starts[STORE_AFTER[i]], starts[i + 1])
+                stored = slice(*STORE_AFTER[i])
                 nc.sync.dma_start(out_words[:, stored], codes[:, stored].bitcast(I32))
 
         weave(0)
@@ -136,6 +133,7 @@ def tile_picked_phput_none_po_kernel(tc, x_words, x_scales, mem, w1, offs, slot,
             weave(i)
             quantise(i - 1)
         quantise(len(CHUNKS) - 1)
+        scale_out = out_2[0].bitcast(I32).rearrange("(q r) (g c) -> q g r c", r=4, g=U // GROUP)
         for q in range(4):
             queue = nc.scalar if q % 2 else nc.sync
-            queue.dma_start(out_2[0, 4 * q : 4 * q + 4, :].bitcast(I32), out_scale[32 * q : 32 * q + 4, :].bitcast(I32))
+            queue.dma_start(scale_out[q], out_scale[32 * q : 32 * q + 16, :].bitcast(I32))

@@ -15,10 +15,12 @@ FP8X4 = mybir.dt.float8_e4m3fn_x4
 
 P = 128
 PACK = 4
+X_FIRST = 512
+HALF = S // 2
+PIECE = 256
 GROUP = 512
-CHUNKS = ((0, 256), (512, 1024), (1024, 1536), (256, 512), (1536, 1792), (1792, 2048))
-SCALAR_FROM = 4
-STORE_AFTER = {2: (512, 1536), 3: (0, 512), 4: (1536, 1792), 5: (1792, 2048)}
+CHUNKS = ((0, 512, "vector"), (512, 1024, "vector"), (1024, 1280, "direct"), (1536, 2048, "scalar"), (1280, 1536, "scalar"))
+STORE_AFTER = {0: (0, 512), 2: (512, 1280), 3: (1536, 2048), 4: (1280, 1536)}
 
 
 def tile_picked_phput_none_po_kernel(tc, x_words, x_scales, mem, w1, offs, slot, out_0, out_1, out_2):
@@ -36,34 +38,36 @@ def tile_picked_phput_none_po_kernel(tc, x_words, x_scales, mem, w1, offs, slot,
         nc.vector.memset(x_scale[:].bitcast(I32), 0)
 
         nc.sync.dma_start(offs_sb[:], offs)
-        scale_rows = x_scales[0].rearrange("(r e) c -> e r c", e=2)
         w_raw = [keep.tile([P, PACK, N // 2], F32, name="w_raw%d" % h, tag="slot%d" % (h + 1), align_bytes=64) for h in range(2)]
         w_rows = w1.rearrange("(p j) n -> p j n", j=PACK)
-        nc.sync.dma_start(w_raw[0][:], w_rows[:, :, 0 : N // 2])
-        for e in range(2):
-            nc.sync.dma_start(scale_table[e:P:16, :].bitcast(I32), scale_rows[e].bitcast(I32))
-        nc.sync.dma_start(w_raw[1][:], w_rows[:, :, N // 2 : N])
         word_table = keep.tile([P, T], U32, name="word_table", tag="slot3", align_bytes=64)
-        nc.sync.dma_start(word_table[:].bitcast(I32), x_words[0].rearrange("p c r -> p (c r)").bitcast(I32))
+        word_rows = x_words[0].rearrange("p c r -> p (c r)").bitcast(I32)
+        nc.sync.dma_start(word_table[:, 0:X_FIRST].bitcast(I32), word_rows[:, 0:X_FIRST])
+        nc.sync.dma_start(scale_table[0:P:8, :].bitcast(I32), x_scales[0].bitcast(I32))
+        nc.sync.dma_start(w_raw[0][:], w_rows[:, :, 0 : N // 2])
+        nc.sync.dma_start(w_raw[1][:], w_rows[:, :, N // 2 : N])
+        nc.sync.dma_start(word_table[:, X_FIRST:T].bitcast(I32), word_rows[:, X_FIRST:T])
         nc.sync.dma_start(slot_sb[:], slot)
 
         picked_scale = keep.tile([P, S], U8, name="picked_scale", align_bytes=64)
         nc.vector.tensor_copy(picked_scale[:], scale_table[:].indirect(offs_sb[:]))
-        for e in range(2):
-            nc.sync.dma_start(x_scale[2 + e : P : 32, :].bitcast(I32), picked_scale[16 + e : P : 32, :].bitcast(I32))
         for q in range(4):
-            nc.vector.tensor_copy(x_scale[32 * q : 32 * q + 2, :].bitcast(I32), picked_scale[32 * q : 32 * q + 2, :].bitcast(I32))
+            nc.sync.dma_start(x_scale[32 * q : 32 * q + 4, :].bitcast(I32), picked_scale[32 * q : 32 * q + 32 : 8, :].bitcast(I32))
 
         w_bf = keep.tile([P, PACK * N], BF16, name="w_bf", align_bytes=64)
-        w_dealt = w_bf[:].rearrange("p (t h m j) -> p h m j t", t=PACK, h=2, j=PACK)
+        w_dealt = w_bf[:].rearrange("p (u e h m j) -> p h u m j e", u=2, e=2, h=2, j=PACK)
         for h in range(2):
-            nc.vector.tensor_copy(w_dealt[:, h], w_raw[h][:].rearrange("p j (m t) -> p m j t", t=PACK))
+            nc.vector.tensor_copy(w_dealt[:, h], w_raw[h][:].rearrange("p j (m u e) -> p u m j e", u=2, e=2))
         w_codes = keep.tile([P, N], U32, name="w_codes", align_bytes=64)
         w_scale = keep.tile([P, N], U8, name="w_scale", align_bytes=64)
         nc.vector.quantize_mx(out=w_codes[:].bitcast(FP8X4), scales=w_scale[:], in_=w_bf[:])
 
         x_codes = keep.tile([P, S], U32, name="x_codes", align_bytes=64)
-        nc.vector.tensor_copy(x_codes[:], word_table[:].indirect(offs_sb[:]))
+        for h in range(2):
+            nc.vector.tensor_copy(
+                x_codes[:, h * HALF : (h + 1) * HALF],
+                word_table[:].indirect(offs_sb[:, h * HALF // 16 : (h + 1) * HALF // 16]),
+            )
 
         mem_rows = mem.rearrange("(p t) c -> t p c", t=PACK)
         out_rows = out_0.rearrange("(p t) c -> t p c", t=PACK)
@@ -75,64 +79,68 @@ def tile_picked_phput_none_po_kernel(tc, x_words, x_scales, mem, w1, offs, slot,
 
         ys = []
         for t in range(PACK):
-            acc = psum.tile([P, S], F32, name="acc%d" % t)
-            cols = slice(t * P, (t + 1) * P)
-            nc.tensor.matmul_mx(
-                out=acc[:],
-                lhsT=w_codes[:, cols].bitcast(FP8X4),
-                lhsT_scale=w_scale[:, cols],
-                rhs=x_codes[:].bitcast(FP8X4),
-                rhs_scale=x_scale[:],
-                start=True,
-                stop=True,
-            )
             y = keep.tile([P, S], F32, name="y%d" % t)
-            nc.scalar.copy(y[:], acc[:])
+            cols = slice(t * P, (t + 1) * P)
+            for lo, hi in ((0, HALF), (HALF, S)) if t == 0 else ((0, S),):
+                acc = psum.tile([P, hi - lo], F32, name="acc%d_%d" % (t, lo))
+                nc.tensor.matmul_mx(
+                    out=acc[:],
+                    lhsT=w_codes[:, cols].bitcast(FP8X4),
+                    lhsT_scale=w_scale[:, cols],
+                    rhs=x_codes[:, lo:hi].bitcast(FP8X4),
+                    rhs_scale=x_scale[:, lo:hi],
+                    start=True,
+                    stop=True,
+                )
+                nc.scalar.copy(y[:, lo:hi], acc[:])
             ys.append(y)
 
-        pairs = [keep.tile([P, PACK * (hi - lo)], BF16, name="pairs%d" % i, align_bytes=64) for i, (lo, hi) in enumerate(CHUNKS)]
+        grouped = [keep.tile([P, PACK * (hi - lo)], BF16, name="grouped%d" % i, align_bytes=64) for i, (lo, hi, how) in enumerate(CHUNKS)]
+        staged = {
+            i: keep.tile([P, PACK * (hi - lo)], BF16, name="staged%d" % i, align_bytes=64)
+            for i, (lo, hi, how) in enumerate(CHUNKS)
+            if how != "direct"
+        }
         for t in range(PACK):
             nc.vector.tensor_copy(windows[t][:].indirect(slot_sb[:]), ys[t][:])
             nc.sync.dma_start(out_rows[t], windows[t][:])
-            for i, (lo, hi) in enumerate(CHUNKS):
-                dst = pairs[i][:].rearrange("p (h c e) -> p h c e", h=2, e=2)[:, t // 2, :, t % 2]
+            for i, (lo, hi, how) in enumerate(CHUNKS):
                 src = windows[t][:, lo:hi]
-                if t >= 2 and i == 0:
-                    nc.vector.tensor_copy(dst, src)
+                if how == "direct":
+                    nc.scalar.copy(grouped[i][:].rearrange("p (c t) -> p t c", t=PACK)[:, t, :], src)
+                elif how == "vector" and t == PACK - 1:
+                    nc.vector.tensor_copy(staged[i][:, t * (hi - lo) : (t + 1) * (hi - lo)], src)
                 else:
-                    nc.scalar.copy(dst, src)
+                    nc.scalar.copy(staged[i][:, t * (hi - lo) : (t + 1) * (hi - lo)], src)
 
         out_scale = keep.tile([P, GROUP], U8, name="out_scale", align_bytes=64)
         codes = keep.tile([P, U], U32, name="codes", align_bytes=64)
         out_words = out_1[0].rearrange("p c r -> p (c r)").bitcast(I32)
-        grouped = [keep.tile([P, PACK * (hi - lo)], BF16, name="grouped%d" % i, align_bytes=64) for i, (lo, hi) in enumerate(CHUNKS)]
 
-        def weave(i):
-            word = U32 if i >= SCALAR_FROM else I32
-            dst = grouped[i][:].bitcast(word).rearrange("p (c h) -> p c h", h=2)
-            src = pairs[i][:].bitcast(word).rearrange("p (h c) -> p c h", h=2)
-            if i >= SCALAR_FROM:
+        for i in staged:
+            dst = grouped[i][:].rearrange("p (c i t) -> p c t i", i=4, t=PACK)
+            src = staged[i][:].rearrange("p (t c i) -> p c t i", i=4, t=PACK)
+            if CHUNKS[i][2] == "scalar":
                 nc.scalar.copy(dst, src)
             else:
                 nc.vector.tensor_copy(dst, src)
 
-        def quantise(i):
-            lo, hi = CHUNKS[i]
-            g = lo // GROUP
-            nc.vector.quantize_mx(
-                out=codes[:, lo:hi].bitcast(FP8X4),
-                scales=out_scale[4 * g : P, lo - g * GROUP : hi - g * GROUP],
-                in_=grouped[i][:],
-            )
+        upper = True
+        for i, (lo, hi, how) in enumerate(CHUNKS):
+            starts = list(range(lo, hi, PIECE))
+            if (lo % GROUP >= PIECE) == upper:
+                starts = starts[::-1]
+            for c in starts:
+                nc.vector.quantize_mx(
+                    out=codes[:, c : c + PIECE].bitcast(FP8X4),
+                    scales=out_scale[4 * (c // GROUP) : P, c % GROUP : c % GROUP + PIECE],
+                    in_=grouped[i][:, PACK * (c - lo) : PACK * (c - lo + PIECE)],
+                )
+            upper = starts[-1] % GROUP >= PIECE
             if i in STORE_AFTER:
                 stored = slice(*STORE_AFTER[i])
                 nc.sync.dma_start(out_words[:, stored], codes[:, stored].bitcast(I32))
 
-        weave(0)
-        for i in range(1, len(CHUNKS)):
-            weave(i)
-            quantise(i - 1)
-        quantise(len(CHUNKS) - 1)
         scale_out = out_2[0].bitcast(I32).rearrange("(q r) (g c) -> q g r c", r=4, g=U // GROUP)
         for q in range(4):
             queue = nc.scalar if q % 2 else nc.sync

@@ -19,8 +19,14 @@ X_FIRST = 512
 HALF = S // 2
 PIECE = 256
 GROUP = 512
-CHUNKS = ((0, 512, "vector"), (512, 1024, "vector"), (1024, 1280, "direct"), (1536, 2048, "scalar"), (1280, 1536, "scalar"))
-STORE_AFTER = {0: (0, 512), 2: (512, 1280), 3: (1536, 2048), 4: (1280, 1536)}
+CHUNKS = (
+    (256, 512, "elements"),
+    (512, 1024, "vector"),
+    (1024, 1536, "vector"),
+    (0, 256, "vector"),
+    (1536, 2048, "scalar"),
+)
+STORES = {768: (256, 1024), 1280: (1024, 1536), 0: (0, 256), 1792: (1792, 2048), 1536: (1536, 1792)}
 
 
 def tile_picked_phput_none_po_kernel(tc, x_words, x_scales, mem, w1, offs, slot, out_0, out_1, out_2):
@@ -32,20 +38,20 @@ def tile_picked_phput_none_po_kernel(tc, x_words, x_scales, mem, w1, offs, slot,
 
         offs_sb = lists.tile([P, S // 16], U16, name="offs_sb")
         slot_sb = lists.tile([P, S // 16], U16, name="slot_sb")
-        scale_table = keep.tile([P, T], U8, name="scale_table", tag="slot0", align_bytes=64)
+        scale_table = keep.tile([P, T], U8, name="scale_table", tag="room0", align_bytes=64)
         x_scale = keep.tile([P, S], U8, name="x_scale", align_bytes=64)
         nc.vector.memset(scale_table[:].bitcast(I32), 0)
         nc.vector.memset(x_scale[:].bitcast(I32), 0)
 
-        nc.sync.dma_start(offs_sb[:], offs)
-        w_raw = [keep.tile([P, PACK, N // 2], F32, name="w_raw%d" % h, tag="slot%d" % (h + 1), align_bytes=64) for h in range(2)]
+        w_raw = [keep.tile([P, 2, N], F32, name="w_raw%d" % h, tag="room%d" % (h + 1), align_bytes=64) for h in range(2)]
         w_rows = w1.rearrange("(p j) n -> p j n", j=PACK)
-        word_table = keep.tile([P, T], U32, name="word_table", tag="slot3", align_bytes=64)
+        word_table = keep.tile([P, T], U32, name="word_table", tag="room3", align_bytes=64)
         word_rows = x_words[0].rearrange("p c r -> p (c r)").bitcast(I32)
+        nc.sync.dma_start(offs_sb[:], offs)
         nc.sync.dma_start(word_table[:, 0:X_FIRST].bitcast(I32), word_rows[:, 0:X_FIRST])
         nc.sync.dma_start(scale_table[0:P:8, :].bitcast(I32), x_scales[0].bitcast(I32))
-        nc.sync.dma_start(w_raw[0][:], w_rows[:, :, 0 : N // 2])
-        nc.sync.dma_start(w_raw[1][:], w_rows[:, :, N // 2 : N])
+        for h in range(2):
+            nc.sync.dma_start(w_raw[h][:], w_rows[:, 2 * h : 2 * h + 2, :])
         nc.sync.dma_start(word_table[:, X_FIRST:T].bitcast(I32), word_rows[:, X_FIRST:T])
         nc.sync.dma_start(slot_sb[:], slot)
 
@@ -55,7 +61,7 @@ def tile_picked_phput_none_po_kernel(tc, x_words, x_scales, mem, w1, offs, slot,
             nc.sync.dma_start(x_scale[32 * q : 32 * q + 4, :].bitcast(I32), picked_scale[32 * q : 32 * q + 32 : 8, :].bitcast(I32))
 
         w_bf = keep.tile([P, PACK * N], BF16, name="w_bf", align_bytes=64)
-        w_dealt = w_bf[:].rearrange("p (u e h m j) -> p h u m j e", u=2, e=2, h=2, j=PACK)
+        w_dealt = w_bf[:].rearrange("p (u e m h j) -> p h u m j e", u=2, e=2, h=2, j=2)
         for h in range(2):
             nc.vector.tensor_copy(w_dealt[:, h], w_raw[h][:].rearrange("p j (m u e) -> p u m j e", u=2, e=2))
         w_codes = keep.tile([P, N], U32, name="w_codes", align_bytes=64)
@@ -63,17 +69,14 @@ def tile_picked_phput_none_po_kernel(tc, x_words, x_scales, mem, w1, offs, slot,
         nc.vector.quantize_mx(out=w_codes[:].bitcast(FP8X4), scales=w_scale[:], in_=w_bf[:])
 
         x_codes = keep.tile([P, S], U32, name="x_codes", align_bytes=64)
-        for h in range(2):
-            nc.vector.tensor_copy(
-                x_codes[:, h * HALF : (h + 1) * HALF],
-                word_table[:].indirect(offs_sb[:, h * HALF // 16 : (h + 1) * HALF // 16]),
-            )
+        for lo in (0, HALF):
+            nc.vector.tensor_copy(x_codes[:, lo : lo + HALF], word_table[:].indirect(offs_sb[:, lo // 16 : (lo + HALF) // 16]))
 
         mem_rows = mem.rearrange("(p t) c -> t p c", t=PACK)
         out_rows = out_0.rearrange("(p t) c -> t p c", t=PACK)
         windows = []
         for t in range(PACK):
-            window = keep.tile([P, U], F32, name="window%d" % t, tag="slot%d" % t, align_bytes=64)
+            window = keep.tile([P, U], F32, name="window%d" % t, tag="room%d" % t, align_bytes=64)
             nc.sync.dma_start(window[:], mem_rows[t])
             windows.append(window)
 
@@ -95,53 +98,68 @@ def tile_picked_phput_none_po_kernel(tc, x_words, x_scales, mem, w1, offs, slot,
                 nc.scalar.copy(y[:, lo:hi], acc[:])
             ys.append(y)
 
-        grouped = [keep.tile([P, PACK * (hi - lo)], BF16, name="grouped%d" % i, align_bytes=64) for i, (lo, hi, how) in enumerate(CHUNKS)]
-        staged = {
-            i: keep.tile([P, PACK * (hi - lo)], BF16, name="staged%d" % i, align_bytes=64)
-            for i, (lo, hi, how) in enumerate(CHUNKS)
-            if how != "direct"
-        }
+        staged = [keep.tile([P, PACK * (hi - lo)], BF16, name="staged%d" % lo, align_bytes=64) for lo, hi, how in CHUNKS]
         for t in range(PACK):
             nc.vector.tensor_copy(windows[t][:].indirect(slot_sb[:]), ys[t][:])
             nc.sync.dma_start(out_rows[t], windows[t][:])
-            for i, (lo, hi, how) in enumerate(CHUNKS):
+            for stage, (lo, hi, how) in zip(staged, CHUNKS):
                 src = windows[t][:, lo:hi]
-                if how == "direct":
-                    nc.scalar.copy(grouped[i][:].rearrange("p (c t) -> p t c", t=PACK)[:, t, :], src)
-                elif how == "vector" and t == PACK - 1:
-                    nc.vector.tensor_copy(staged[i][:, t * (hi - lo) : (t + 1) * (hi - lo)], src)
+                if how != "elements":
+                    nc.scalar.copy(stage[:].rearrange("p (h c e) -> p h e c", h=2, e=2)[:, t // 2, t % 2, :], src)
+                elif t < PACK - 1:
+                    nc.scalar.copy(stage[:, t * (hi - lo) : (t + 1) * (hi - lo)], src)
                 else:
-                    nc.scalar.copy(staged[i][:, t * (hi - lo) : (t + 1) * (hi - lo)], src)
+                    nc.vector.tensor_copy(stage[:, t * (hi - lo) : (t + 1) * (hi - lo)], src)
 
         out_scale = keep.tile([P, GROUP], U8, name="out_scale", align_bytes=64)
         codes = keep.tile([P, U], U32, name="codes", align_bytes=64)
         out_words = out_1[0].rearrange("p c r -> p (c r)").bitcast(I32)
 
-        for i in staged:
-            dst = grouped[i][:].rearrange("p (c i t) -> p c t i", i=4, t=PACK)
-            src = staged[i][:].rearrange("p (t c i) -> p c t i", i=4, t=PACK)
-            if CHUNKS[i][2] == "scalar":
-                nc.scalar.copy(dst, src)
+        def weave(stage, lo, hi, how, pieces):
+            if how == "scalar":
+                woven = {}
+                for c in pieces:
+                    grouped = keep.tile([P, PACK * PIECE], BF16, name="grouped%d" % c, align_bytes=64)
+                    words = stage[:].bitcast(U32).rearrange("p (h c) -> p c h", h=2)
+                    nc.scalar.copy(grouped[:].bitcast(U32).rearrange("p (c h) -> p c h", h=2), words[:, c - lo : c - lo + PIECE, :])
+                    woven[c] = grouped[:]
+                return woven
+            grouped = keep.tile([P, PACK * (hi - lo)], BF16, name="grouped%d" % lo, align_bytes=64)
+            if how == "vector":
+                nc.vector.tensor_copy(
+                    grouped[:].bitcast(I32).rearrange("p (c h) -> p c h", h=2),
+                    stage[:].bitcast(I32).rearrange("p (h c) -> p c h", h=2),
+                )
             else:
-                nc.vector.tensor_copy(dst, src)
+                nc.vector.tensor_copy(
+                    grouped[:].rearrange("p (c i t) -> p c t i", i=4, t=PACK),
+                    stage[:].rearrange("p (t c i) -> p c t i", i=4, t=PACK),
+                )
+            return {c: grouped[:, PACK * (c - lo) : PACK * (c - lo + PIECE)] for c in pieces}
 
-        upper = True
-        for i, (lo, hi, how) in enumerate(CHUNKS):
-            starts = list(range(lo, hi, PIECE))
-            if (lo % GROUP >= PIECE) == upper:
-                starts = starts[::-1]
-            for c in starts:
+        def quantise(woven):
+            for c in woven:
                 nc.vector.quantize_mx(
                     out=codes[:, c : c + PIECE].bitcast(FP8X4),
                     scales=out_scale[4 * (c // GROUP) : P, c % GROUP : c % GROUP + PIECE],
-                    in_=grouped[i][:, PACK * (c - lo) : PACK * (c - lo + PIECE)],
+                    in_=woven[c],
                 )
-            upper = starts[-1] % GROUP >= PIECE
-            if i in STORE_AFTER:
-                stored = slice(*STORE_AFTER[i])
-                nc.sync.dma_start(out_words[:, stored], codes[:, stored].bitcast(I32))
+                if c in STORES:
+                    stored = slice(*STORES[c])
+                    nc.sync.dma_start(out_words[:, stored], codes[:, stored].bitcast(I32))
+
+        waiting = {}
+        last_half = None
+        for stage, (lo, hi, how) in zip(staged, CHUNKS):
+            pieces = list(range(lo, hi, PIECE))
+            if pieces[0] % GROUP == last_half:
+                pieces = pieces[::-1]
+            last_half = pieces[-1] % GROUP
+            woven = weave(stage, lo, hi, how, pieces)
+            quantise(waiting)
+            waiting = woven
+        quantise(waiting)
 
         scale_out = out_2[0].bitcast(I32).rearrange("(q r) (g c) -> q g r c", r=4, g=U // GROUP)
         for q in range(4):
-            queue = nc.scalar if q % 2 else nc.sync
-            queue.dma_start(scale_out[q], out_scale[32 * q : 32 * q + 16, :].bitcast(I32))
+            nc.sync.dma_start(scale_out[q], out_scale[32 * q : 32 * q + 16, :].bitcast(I32))

@@ -19,14 +19,7 @@ X_FIRST = 512
 HALF = S // 2
 PIECE = 256
 GROUP = 512
-CHUNKS = (
-    (256, 512, "elements"),
-    (512, 1024, "vector"),
-    (1024, 1536, "vector"),
-    (0, 256, "vector"),
-    (1536, 2048, "scalar"),
-)
-STORES = {768: (256, 1024), 1280: (1024, 1536), 0: (0, 256), 1792: (1792, 2048), 1536: (1536, 1792)}
+SPLIT = 1024
 
 
 def tile_picked_phput_none_po_kernel(tc, x_words, x_scales, mem, w1, offs, slot, out_0, out_1, out_2):
@@ -98,67 +91,50 @@ def tile_picked_phput_none_po_kernel(tc, x_words, x_scales, mem, w1, offs, slot,
                 nc.scalar.copy(y[:, lo:hi], acc[:])
             ys.append(y)
 
-        staged = [keep.tile([P, PACK * (hi - lo)], BF16, name="staged%d" % lo, align_bytes=64) for lo, hi, how in CHUNKS]
-        for t in range(PACK):
-            nc.vector.tensor_copy(windows[t][:].indirect(slot_sb[:]), ys[t][:])
-            nc.sync.dma_start(out_rows[t], windows[t][:])
-            for stage, (lo, hi, how) in zip(staged, CHUNKS):
-                src = windows[t][:, lo:hi]
-                if how != "elements":
-                    nc.scalar.copy(stage[:].rearrange("p (h c e) -> p h e c", h=2, e=2)[:, t // 2, t % 2, :], src)
-                elif t < PACK - 1:
-                    nc.scalar.copy(stage[:, t * (hi - lo) : (t + 1) * (hi - lo)], src)
-                else:
-                    nc.vector.tensor_copy(stage[:, t * (hi - lo) : (t + 1) * (hi - lo)], src)
-
+        grouped = keep.tile([P, PACK * U], BF16, name="grouped", align_bytes=64)
+        by_plane = grouped[:].rearrange("p (c t) -> p t c", t=PACK)
         out_scale = keep.tile([P, GROUP], U8, name="out_scale", align_bytes=64)
         codes = keep.tile([P, U], U32, name="codes", align_bytes=64)
         out_words = out_1[0].rearrange("p c r -> p (c r)").bitcast(I32)
+        mult, add = mybir.AluOpType.mult, mybir.AluOpType.add
 
-        def weave(stage, lo, hi, how, pieces):
-            if how == "scalar":
-                woven = {}
-                for c in pieces:
-                    grouped = keep.tile([P, PACK * PIECE], BF16, name="grouped%d" % c, align_bytes=64)
-                    words = stage[:].bitcast(U32).rearrange("p (h c) -> p c h", h=2)
-                    nc.scalar.copy(grouped[:].bitcast(U32).rearrange("p (c h) -> p c h", h=2), words[:, c - lo : c - lo + PIECE, :])
-                    woven[c] = grouped[:]
-                return woven
-            grouped = keep.tile([P, PACK * (hi - lo)], BF16, name="grouped%d" % lo, align_bytes=64)
-            if how == "vector":
-                nc.vector.tensor_copy(
-                    grouped[:].bitcast(I32).rearrange("p (c h) -> p c h", h=2),
-                    stage[:].bitcast(I32).rearrange("p (h c) -> p c h", h=2),
-                )
-            else:
-                nc.vector.tensor_copy(
-                    grouped[:].rearrange("p (c i t) -> p c t i", i=4, t=PACK),
-                    stage[:].rearrange("p (t c i) -> p c t i", i=4, t=PACK),
-                )
-            return {c: grouped[:, PACK * (c - lo) : PACK * (c - lo + PIECE)] for c in pieces}
+        def quantise(k):
+            lo, hi = k * PIECE, (k + 1) * PIECE
+            nc.vector.quantize_mx(
+                out=codes[:, lo:hi].bitcast(FP8X4),
+                scales=out_scale[4 * (lo // GROUP) : P, lo % GROUP : lo % GROUP + PIECE],
+                in_=grouped[:, PACK * lo : PACK * hi],
+            )
 
-        def quantise(woven):
-            for c in woven:
-                nc.vector.quantize_mx(
-                    out=codes[:, c : c + PIECE].bitcast(FP8X4),
-                    scales=out_scale[4 * (c // GROUP) : P, c % GROUP : c % GROUP + PIECE],
-                    in_=woven[c],
-                )
-                if c in STORES:
-                    stored = slice(*STORES[c])
-                    nc.sync.dma_start(out_words[:, stored], codes[:, stored].bitcast(I32))
+        def store(lo, hi):
+            nc.sync.dma_start(out_words[:, lo:hi], codes[:, lo:hi].bitcast(I32))
 
-        waiting = {}
-        last_half = None
-        for stage, (lo, hi, how) in zip(staged, CHUNKS):
-            pieces = list(range(lo, hi, PIECE))
-            if pieces[0] % GROUP == last_half:
-                pieces = pieces[::-1]
-            last_half = pieces[-1] % GROUP
-            woven = weave(stage, lo, hi, how, pieces)
-            quantise(waiting)
-            waiting = woven
-        quantise(waiting)
+        for t in range(PACK):
+            nc.vector.tensor_copy(windows[t][:].indirect(slot_sb[:]), ys[t][:])
+            nc.sync.dma_start(out_rows[t], windows[t][:])
+            if t < 2:
+                nc.gpsimd.tensor_scalar(by_plane[:, t, 0:SPLIT], windows[t][:, 0:SPLIT], 1.0, 0.0, mult, add)
+            elif t == 2:
+                both = grouped[:, 0 : PACK * SPLIT].rearrange("p (c t) -> p c t", t=PACK)[:, :, 2:4]
+                nc.gpsimd.tensor_scalar(both, windows[t][:, 0:SPLIT].unsqueeze(2).to_broadcast([P, SPLIT, 2]), 1.0, 0.0, mult, add)
+            if t < 3:
+                nc.scalar.copy(by_plane[:, t, SPLIT:U], windows[t][:, SPLIT:U])
+
+        for lo in range(SPLIT, U, PIECE):
+            nc.scalar.copy(by_plane[:, 3, lo : lo + PIECE], windows[3][:, lo : lo + PIECE])
+        for k in range(4):
+            nc.vector.tensor_copy(by_plane[:, 3, k * PIECE : (k + 1) * PIECE], windows[3][:, k * PIECE : (k + 1) * PIECE])
+            if k:
+                quantise(k - 1)
+        store(0, 768)
+        quantise(4)
+        quantise(3)
+        store(768, 1280)
+        quantise(5)
+        quantise(6)
+        store(1280, 1792)
+        quantise(7)
+        store(1792, 2048)
 
         scale_out = out_2[0].bitcast(I32).rearrange("(q r) (g c) -> q g r c", r=4, g=U // GROUP)
         for q in range(4):

@@ -15,11 +15,11 @@ FP8X4 = mybir.dt.float8_e4m3fn_x4
 
 P = 128
 PACK = 4
-X_FIRST = 512
+X_FIRST = 768
 HALF = S // 2
 PIECE = 256
 GROUP = 512
-SPLIT = 1024
+STORES = {3: (512, 1024), 5: (1024, 1536), 6: (1536, 1792), 7: (1792, 2048)}
 
 
 def tile_picked_phput_none_po_kernel(tc, x_words, x_scales, mem, w1, offs, slot, out_0, out_1, out_2):
@@ -40,8 +40,8 @@ def tile_picked_phput_none_po_kernel(tc, x_words, x_scales, mem, w1, offs, slot,
         w_rows = w1.rearrange("(p j) n -> p j n", j=PACK)
         word_table = keep.tile([P, T], U32, name="word_table", tag="room3", align_bytes=64)
         word_rows = x_words[0].rearrange("p c r -> p (c r)").bitcast(I32)
-        nc.sync.dma_start(offs_sb[:], offs)
         nc.sync.dma_start(word_table[:, 0:X_FIRST].bitcast(I32), word_rows[:, 0:X_FIRST])
+        nc.sync.dma_start(offs_sb[:], offs)
         nc.sync.dma_start(scale_table[0:P:8, :].bitcast(I32), x_scales[0].bitcast(I32))
         for h in range(2):
             nc.sync.dma_start(w_raw[h][:], w_rows[:, 2 * h : 2 * h + 2, :])
@@ -93,6 +93,10 @@ def tile_picked_phput_none_po_kernel(tc, x_words, x_scales, mem, w1, offs, slot,
 
         grouped = keep.tile([P, PACK * U], BF16, name="grouped", align_bytes=64)
         by_plane = grouped[:].rearrange("p (c t) -> p t c", t=PACK)
+        by_column = grouped[:].rearrange("p (c t) -> p c t", t=PACK)
+        pairs = keep.tile([P, PACK * 3 * PIECE], BF16, name="pairs", align_bytes=64)
+        pair_planes = pairs[:].rearrange("p (k h c e) -> p h e k c", k=3, h=2, e=2)
+        pair_words = pairs[:].bitcast(I32).rearrange("p (k h c) -> p k c h", k=3, h=2)
         out_scale = keep.tile([P, GROUP], U8, name="out_scale", align_bytes=64)
         codes = keep.tile([P, U], U32, name="codes", align_bytes=64)
         out_words = out_1[0].rearrange("p c r -> p (c r)").bitcast(I32)
@@ -112,29 +116,31 @@ def tile_picked_phput_none_po_kernel(tc, x_words, x_scales, mem, w1, offs, slot,
         for t in range(PACK):
             nc.vector.tensor_copy(windows[t][:].indirect(slot_sb[:]), ys[t][:])
             nc.sync.dma_start(out_rows[t], windows[t][:])
-            if t < 2:
-                nc.gpsimd.tensor_scalar(by_plane[:, t, 0:SPLIT], windows[t][:, 0:SPLIT], 1.0, 0.0, mult, add)
-            elif t == 2:
-                both = grouped[:, 0 : PACK * SPLIT].rearrange("p (c t) -> p c t", t=PACK)[:, :, 2:4]
-                nc.gpsimd.tensor_scalar(both, windows[t][:, 0:SPLIT].unsqueeze(2).to_broadcast([P, SPLIT, 2]), 1.0, 0.0, mult, add)
+            for lo, hi in ((0, 512), (1280, 1536)):
+                if t < 2:
+                    nc.gpsimd.tensor_scalar(by_plane[:, t, lo:hi], windows[t][:, lo:hi], 1.0, 0.0, mult, add)
+                elif t == 2:
+                    nc.gpsimd.tensor_scalar(by_column[:, lo:hi, 2:4], windows[t][:, lo:hi].unsqueeze(2).to_broadcast([P, hi - lo, 2]), 1.0, 0.0, mult, add)
+            nc.scalar.copy(pair_planes[:, t // 2, t % 2], windows[t][:, 512:1280].rearrange("p (k c) -> p k c", k=3))
             if t < 3:
-                nc.scalar.copy(by_plane[:, t, SPLIT:U], windows[t][:, SPLIT:U])
+                nc.scalar.copy(by_plane[:, t, 1536:U], windows[t][:, 1536:U])
 
-        for lo in range(SPLIT, U, PIECE):
+        for lo in range(1280, U, PIECE):
             nc.scalar.copy(by_plane[:, 3, lo : lo + PIECE], windows[3][:, lo : lo + PIECE])
-        for k in range(4):
+        for k in range(2):
             nc.vector.tensor_copy(by_plane[:, 3, k * PIECE : (k + 1) * PIECE], windows[3][:, k * PIECE : (k + 1) * PIECE])
-            if k:
-                quantise(k - 1)
-        store(0, 768)
-        quantise(4)
-        quantise(3)
-        store(768, 1280)
-        quantise(5)
-        quantise(6)
-        store(1280, 1792)
-        quantise(7)
-        store(1792, 2048)
+        quantise(0)
+        quantise(1)
+        store(0, 512)
+        for k in range(3):
+            nc.vector.tensor_copy(
+                grouped[:, PACK * PIECE * (k + 2) : PACK * PIECE * (k + 3)].bitcast(I32).rearrange("p (c h) -> p c h", h=2),
+                pair_words[:, k],
+            )
+        for k in range(2, 8):
+            quantise(k)
+            if k in STORES:
+                store(*STORES[k])
 
         scale_out = out_2[0].bitcast(I32).rearrange("(q r) (g c) -> q g r c", r=4, g=U // GROUP)
         for q in range(4):

@@ -15,11 +15,10 @@ FP8X4 = mybir.dt.float8_e4m3fn_x4
 
 P = 128
 PACK = 4
-X_FIRST = 768
 HALF = S // 2
 PIECE = 256
 GROUP = 512
-STORES = {3: (512, 1024), 5: (1024, 1536), 6: (1536, 1792), 7: (1792, 2048)}
+STORES = {3: (512, 1024), 5: (1024, 1536), 7: (1536, 2048)}
 
 
 def tile_picked_phput_none_po_kernel(tc, x_words, x_scales, mem, w1, offs, slot, out_0, out_1, out_2):
@@ -36,16 +35,15 @@ def tile_picked_phput_none_po_kernel(tc, x_words, x_scales, mem, w1, offs, slot,
         nc.vector.memset(scale_table[:].bitcast(I32), 0)
         nc.vector.memset(x_scale[:].bitcast(I32), 0)
 
-        w_raw = [keep.tile([P, 2, N], F32, name="w_raw%d" % h, tag="room%d" % (h + 1), align_bytes=64) for h in range(2)]
+        w_raw = keep.tile([P, PACK, N], F32, name="w_raw", tag="room1", align_bytes=64)
         w_rows = w1.rearrange("(p j) n -> p j n", j=PACK)
         word_table = keep.tile([P, T], U32, name="word_table", tag="room3", align_bytes=64)
         word_rows = x_words[0].rearrange("p c r -> p (c r)").bitcast(I32)
-        nc.sync.dma_start(word_table[:, 0:X_FIRST].bitcast(I32), word_rows[:, 0:X_FIRST])
+        nc.sync.dma_start(w_raw[:, 0:1, :], w_rows[:, 0:1, :])
         nc.sync.dma_start(offs_sb[:], offs)
         nc.sync.dma_start(scale_table[0:P:8, :].bitcast(I32), x_scales[0].bitcast(I32))
-        for h in range(2):
-            nc.sync.dma_start(w_raw[h][:], w_rows[:, 2 * h : 2 * h + 2, :])
-        nc.sync.dma_start(word_table[:, X_FIRST:T].bitcast(I32), word_rows[:, X_FIRST:T])
+        nc.sync.dma_start(w_raw[:, 1:PACK, :], w_rows[:, 1:PACK, :])
+        nc.sync.dma_start(word_table[:].bitcast(I32), word_rows)
         nc.sync.dma_start(slot_sb[:], slot)
 
         picked_scale = keep.tile([P, S], U8, name="picked_scale", align_bytes=64)
@@ -53,10 +51,9 @@ def tile_picked_phput_none_po_kernel(tc, x_words, x_scales, mem, w1, offs, slot,
         for q in range(4):
             nc.sync.dma_start(x_scale[32 * q : 32 * q + 4, :].bitcast(I32), picked_scale[32 * q : 32 * q + 32 : 8, :].bitcast(I32))
 
-        w_bf = keep.tile([P, PACK * N], BF16, name="w_bf", align_bytes=64)
-        w_dealt = w_bf[:].rearrange("p (u e m h j) -> p h u m j e", u=2, e=2, h=2, j=2)
-        for h in range(2):
-            nc.vector.tensor_copy(w_dealt[:, h], w_raw[h][:].rearrange("p j (m u e) -> p u m j e", u=2, e=2))
+        w_bf = keep.tile([P, PACK * N], BF16, name="w_bf", tag="room2", align_bytes=64)
+        w_dealt = w_bf[:].rearrange("p (t m j) -> p m t j", t=PACK, j=PACK)
+        nc.vector.tensor_copy(w_dealt, w_raw[:].rearrange("p j (m t) -> p m t j", t=PACK))
         w_codes = keep.tile([P, N], U32, name="w_codes", align_bytes=64)
         w_scale = keep.tile([P, N], U8, name="w_scale", align_bytes=64)
         nc.vector.quantize_mx(out=w_codes[:].bitcast(FP8X4), scales=w_scale[:], in_=w_bf[:])

@@ -74,7 +74,7 @@ def tile_picked_phput_none_po_kernel(tc, x_words, x_scales, mem, w1, offs, slot,
         for t in range(PACK):
             y = keep.tile([P, S], F32, name="y%d" % t)
             cols = slice(t * P, (t + 1) * P)
-            for lo, hi in ((0, HALF), (HALF, S)) if t == 0 else ((0, S),):
+            for lo, hi in ((0, HALF), (HALF, HALF + P), (HALF + P, S)) if t == 0 else ((0, S),):
                 acc = psum.tile([P, hi - lo], F32, name="acc%d_%d" % (t, lo))
                 nc.tensor.matmul_mx(
                     out=acc[:],
@@ -91,9 +91,9 @@ def tile_picked_phput_none_po_kernel(tc, x_words, x_scales, mem, w1, offs, slot,
         grouped = keep.tile([P, PACK * U], BF16, name="grouped", align_bytes=64)
         by_plane = grouped[:].rearrange("p (c t) -> p t c", t=PACK)
         by_column = grouped[:].rearrange("p (c t) -> p c t", t=PACK)
-        pairs = keep.tile([P, PACK * 3 * PIECE], BF16, name="pairs", align_bytes=64)
-        pair_planes = pairs[:].rearrange("p (k h c e) -> p h e k c", k=3, h=2, e=2)
-        pair_words = pairs[:].bitcast(I32).rearrange("p (k h c) -> p k c h", k=3, h=2)
+        pairs = keep.tile([P, PACK * 2 * PIECE], BF16, name="pairs", align_bytes=64)
+        pair_planes = pairs[:].rearrange("p (k h c e) -> p h e k c", k=2, h=2, e=2)
+        pair_words = pairs[:].bitcast(I32).rearrange("p (k h c) -> p k c h", k=2, h=2)
         out_scale = keep.tile([P, GROUP], U8, name="out_scale", align_bytes=64)
         codes = keep.tile([P, U], U32, name="codes", align_bytes=64)
         out_words = out_1[0].rearrange("p c r -> p (c r)").bitcast(I32)
@@ -113,23 +113,23 @@ def tile_picked_phput_none_po_kernel(tc, x_words, x_scales, mem, w1, offs, slot,
         for t in range(PACK):
             nc.vector.tensor_copy(windows[t][:].indirect(slot_sb[:]), ys[t][:])
             nc.sync.dma_start(out_rows[t], windows[t][:])
-            for lo, hi in ((0, 512), (1280, 1536)):
+            for lo, hi in ((0, 512), (1024, 1408)):
                 if t < 2:
                     nc.gpsimd.tensor_scalar(by_plane[:, t, lo:hi], windows[t][:, lo:hi], 1.0, 0.0, mult, add)
                 elif t == 2:
                     nc.gpsimd.tensor_scalar(by_column[:, lo:hi, 2:4], windows[t][:, lo:hi].unsqueeze(2).to_broadcast([P, hi - lo, 2]), 1.0, 0.0, mult, add)
-            nc.scalar.copy(pair_planes[:, t // 2, t % 2], windows[t][:, 512:1280].rearrange("p (k c) -> p k c", k=3))
+            nc.scalar.copy(pair_planes[:, t // 2, t % 2], windows[t][:, 512:1024].rearrange("p (k c) -> p k c", k=2))
             if t < 3:
-                nc.scalar.copy(by_plane[:, t, 1536:U], windows[t][:, 1536:U])
+                nc.scalar.copy(by_plane[:, t, 1408:U], windows[t][:, 1408:U])
 
-        for lo in range(1280, U, PIECE):
-            nc.scalar.copy(by_plane[:, 3, lo : lo + PIECE], windows[3][:, lo : lo + PIECE])
-        for k in range(2):
-            nc.vector.tensor_copy(by_plane[:, 3, k * PIECE : (k + 1) * PIECE], windows[3][:, k * PIECE : (k + 1) * PIECE])
+        for lo, hi in ((1152, 1280), (1280, 1536), (1536, 1792), (1792, 2048)):
+            nc.scalar.copy(by_plane[:, 3, lo:hi], windows[3][:, lo:hi])
+        for lo, hi in ((0, 256), (256, 512), (1024, 1152)):
+            nc.vector.tensor_copy(by_plane[:, 3, lo:hi], windows[3][:, lo:hi])
         quantise(0)
         quantise(1)
         store(0, 512)
-        for k in range(3):
+        for k in range(2):
             nc.vector.tensor_copy(
                 grouped[:, PACK * PIECE * (k + 2) : PACK * PIECE * (k + 3)].bitcast(I32).rearrange("p (c h) -> p c h", h=2),
                 pair_words[:, k],

@@ -18,7 +18,15 @@ PACK = 4
 HALF = S // 2
 PIECE = 256
 GROUP = 512
-STORES = {3: (512, 1024), 5: (1024, 1536), 7: (1536, 2048)}
+
+FIRST_PASSES = ((0, HALF), (HALF, HALF + P), (HALF + P, S))
+
+GPSIMD_IN_PLACE = ((0, 512), (1024, 1408))
+SCALAR_PAIRS = (512, 1024)
+SCALAR_IN_PLACE = (1408, 2048)
+
+VECTOR_LAST = ((0, 256), (256, 512), (1024, 1152))
+SCALAR_LAST = ((1152, 1280), (1280, 1536), (1536, 1792), (1792, 2048))
 
 
 def tile_picked_phput_none_po_kernel(tc, x_words, x_scales, mem, w1, offs, slot, out_0, out_1, out_2):
@@ -74,7 +82,7 @@ def tile_picked_phput_none_po_kernel(tc, x_words, x_scales, mem, w1, offs, slot,
         for t in range(PACK):
             y = keep.tile([P, S], F32, name="y%d" % t)
             cols = slice(t * P, (t + 1) * P)
-            for lo, hi in ((0, HALF), (HALF, HALF + P), (HALF + P, S)) if t == 0 else ((0, S),):
+            for lo, hi in FIRST_PASSES if t == 0 else ((0, S),):
                 acc = psum.tile([P, hi - lo], F32, name="acc%d_%d" % (t, lo))
                 nc.tensor.matmul_mx(
                     out=acc[:],
@@ -88,56 +96,57 @@ def tile_picked_phput_none_po_kernel(tc, x_words, x_scales, mem, w1, offs, slot,
                 nc.scalar.copy(y[:, lo:hi], acc[:])
             ys.append(y)
 
+        pair_lo, pair_hi = SCALAR_PAIRS
+        pair_pieces = (pair_hi - pair_lo) // PIECE
         grouped = keep.tile([P, PACK * U], BF16, name="grouped", align_bytes=64)
         by_plane = grouped[:].rearrange("p (c t) -> p t c", t=PACK)
         by_column = grouped[:].rearrange("p (c t) -> p c t", t=PACK)
-        pairs = keep.tile([P, PACK * 2 * PIECE], BF16, name="pairs", align_bytes=64)
-        pair_planes = pairs[:].rearrange("p (k h c e) -> p h e k c", k=2, h=2, e=2)
-        pair_words = pairs[:].bitcast(I32).rearrange("p (k h c) -> p k c h", k=2, h=2)
+        pairs = keep.tile([P, PACK * (pair_hi - pair_lo)], BF16, name="pairs", align_bytes=64)
+        pair_planes = pairs[:].rearrange("p (k h c e) -> p h e k c", k=pair_pieces, h=2, e=2)
+        pair_values = pairs[:].bitcast(I32).rearrange("p (k h c) -> p k c h", k=pair_pieces, h=2)
         out_scale = keep.tile([P, GROUP], U8, name="out_scale", align_bytes=64)
         codes = keep.tile([P, U], U32, name="codes", align_bytes=64)
         out_words = out_1[0].rearrange("p c r -> p (c r)").bitcast(I32)
         mult, add = mybir.AluOpType.mult, mybir.AluOpType.add
 
-        def quantise(k):
-            lo, hi = k * PIECE, (k + 1) * PIECE
-            nc.vector.quantize_mx(
-                out=codes[:, lo:hi].bitcast(FP8X4),
-                scales=out_scale[4 * (lo // GROUP) : P, lo % GROUP : lo % GROUP + PIECE],
-                in_=grouped[:, PACK * lo : PACK * hi],
-            )
-
-        def store(lo, hi):
-            nc.sync.dma_start(out_words[:, lo:hi], codes[:, lo:hi].bitcast(I32))
+        def quantise_group(g):
+            for lo in range(g * GROUP, (g + 1) * GROUP, PIECE):
+                nc.vector.quantize_mx(
+                    out=codes[:, lo : lo + PIECE].bitcast(FP8X4),
+                    scales=out_scale[4 * g : P, lo % GROUP : lo % GROUP + PIECE],
+                    in_=grouped[:, PACK * lo : PACK * (lo + PIECE)],
+                )
+            stored = slice(g * GROUP, (g + 1) * GROUP)
+            nc.sync.dma_start(out_words[:, stored], codes[:, stored].bitcast(I32))
 
         for t in range(PACK):
             nc.vector.tensor_copy(windows[t][:].indirect(slot_sb[:]), ys[t][:])
             nc.sync.dma_start(out_rows[t], windows[t][:])
-            for lo, hi in ((0, 512), (1024, 1408)):
+            for lo, hi in GPSIMD_IN_PLACE:
                 if t < 2:
-                    nc.gpsimd.tensor_scalar(by_plane[:, t, lo:hi], windows[t][:, lo:hi], 1.0, 0.0, mult, add)
+                    nc.gpsimd.tensor_scalar(by_plane[:, t, lo:hi], windows[t][:, lo:hi], 1.0, -0.0, mult, add)
                 elif t == 2:
-                    nc.gpsimd.tensor_scalar(by_column[:, lo:hi, 2:4], windows[t][:, lo:hi].unsqueeze(2).to_broadcast([P, hi - lo, 2]), 1.0, 0.0, mult, add)
-            nc.scalar.copy(pair_planes[:, t // 2, t % 2], windows[t][:, 512:1024].rearrange("p (k c) -> p k c", k=2))
-            if t < 3:
-                nc.scalar.copy(by_plane[:, t, 1408:U], windows[t][:, 1408:U])
+                    twice = windows[t][:, lo:hi].unsqueeze(2).to_broadcast([P, hi - lo, 2])
+                    nc.gpsimd.tensor_scalar(by_column[:, lo:hi, 2:4], twice, 1.0, -0.0, mult, add)
+            nc.scalar.copy(pair_planes[:, t // 2, t % 2], windows[t][:, pair_lo:pair_hi].rearrange("p (k c) -> p k c", k=pair_pieces))
+            if t < PACK - 1:
+                lo, hi = SCALAR_IN_PLACE
+                nc.scalar.copy(by_plane[:, t, lo:hi], windows[t][:, lo:hi])
 
-        for lo, hi in ((1152, 1280), (1280, 1536), (1536, 1792), (1792, 2048)):
-            nc.scalar.copy(by_plane[:, 3, lo:hi], windows[3][:, lo:hi])
-        for lo, hi in ((0, 256), (256, 512), (1024, 1152)):
-            nc.vector.tensor_copy(by_plane[:, 3, lo:hi], windows[3][:, lo:hi])
-        quantise(0)
-        quantise(1)
-        store(0, 512)
-        for k in range(2):
+        last = PACK - 1
+        for lo, hi in SCALAR_LAST:
+            nc.scalar.copy(by_plane[:, last, lo:hi], windows[last][:, lo:hi])
+        for lo, hi in VECTOR_LAST:
+            nc.vector.tensor_copy(by_plane[:, last, lo:hi], windows[last][:, lo:hi])
+        quantise_group(0)
+        for k in range(pair_pieces):
+            lo = pair_lo + k * PIECE
             nc.vector.tensor_copy(
-                grouped[:, PACK * PIECE * (k + 2) : PACK * PIECE * (k + 3)].bitcast(I32).rearrange("p (c h) -> p c h", h=2),
-                pair_words[:, k],
+                grouped[:, PACK * lo : PACK * (lo + PIECE)].bitcast(I32).rearrange("p (c h) -> p c h", h=2),
+                pair_values[:, k],
             )
-        for k in range(2, 8):
-            quantise(k)
-            if k in STORES:
-                store(*STORES[k])
+        for g in range(1, U // GROUP):
+            quantise_group(g)
 
         scale_out = out_2[0].bitcast(I32).rearrange("(q r) (g c) -> q g r c", r=4, g=U // GROUP)
         for q in range(4):

@@ -21,12 +21,14 @@ GROUP = 512
 
 FIRST_PASSES = ((0, HALF), (HALF, HALF + P), (HALF + P, S))
 
-GPSIMD_IN_PLACE = ((0, 512), (1024, 1408))
-SCALAR_PAIRS = (512, 1024)
-SCALAR_IN_PLACE = (1408, 2048)
+GPSIMD_IN_PLACE = ((0, 512), (1536, 1920))
+SCALAR_PAIRS = (1024, 1536)
+SCALAR_IN_PLACE = ((512, 1024), (1920, 2048))
 
-VECTOR_LAST = ((0, 256), (256, 512), (1024, 1152))
-SCALAR_LAST = ((1152, 1280), (1280, 1536), (1536, 1792), (1792, 2048))
+VECTOR_LAST = ((0, 256), (256, 512), (1536, 1664))
+SCALAR_LAST_EARLY = ((512, 768), (768, 1024))
+SCALAR_LAST_LATE = ((1664, 1792), (1792, 2048))
+WORD_STORES = ((0, 1024), (1024, 1536), (1536, 2048))
 
 
 def tile_picked_phput_none_po_kernel(tc, x_words, x_scales, mem, w1, offs, slot, out_0, out_1, out_2):
@@ -109,15 +111,14 @@ def tile_picked_phput_none_po_kernel(tc, x_words, x_scales, mem, w1, offs, slot,
         out_words = out_1[0].rearrange("p c r -> p (c r)").bitcast(I32)
         mult, add = mybir.AluOpType.mult, mybir.AluOpType.add
 
-        def quantise_group(g):
-            for lo in range(g * GROUP, (g + 1) * GROUP, PIECE):
+        def quantise_and_store(first, end):
+            for lo in range(first, end, PIECE):
                 nc.vector.quantize_mx(
                     out=codes[:, lo : lo + PIECE].bitcast(FP8X4),
-                    scales=out_scale[4 * g : P, lo % GROUP : lo % GROUP + PIECE],
+                    scales=out_scale[4 * (lo // GROUP) : P, lo % GROUP : lo % GROUP + PIECE],
                     in_=grouped[:, PACK * lo : PACK * (lo + PIECE)],
                 )
-            stored = slice(g * GROUP, (g + 1) * GROUP)
-            nc.sync.dma_start(out_words[:, stored], codes[:, stored].bitcast(I32))
+            nc.sync.dma_start(out_words[:, first:end], codes[:, first:end].bitcast(I32))
 
         for t in range(PACK):
             nc.vector.tensor_copy(windows[t][:].indirect(slot_sb[:]), ys[t][:])
@@ -128,25 +129,32 @@ def tile_picked_phput_none_po_kernel(tc, x_words, x_scales, mem, w1, offs, slot,
                 elif t == 2:
                     twice = windows[t][:, lo:hi].unsqueeze(2).to_broadcast([P, hi - lo, 2])
                     nc.gpsimd.tensor_scalar(by_column[:, lo:hi, 2:4], twice, 1.0, -0.0, mult, add)
-            nc.scalar.copy(pair_planes[:, t // 2, t % 2], windows[t][:, pair_lo:pair_hi].rearrange("p (k c) -> p k c", k=pair_pieces))
             if t < PACK - 1:
-                lo, hi = SCALAR_IN_PLACE
-                nc.scalar.copy(by_plane[:, t, lo:hi], windows[t][:, lo:hi])
+                nc.scalar.copy(pair_planes[:, t // 2, t % 2], windows[t][:, pair_lo:pair_hi].rearrange("p (k c) -> p k c", k=pair_pieces))
+                for lo, hi in SCALAR_IN_PLACE:
+                    nc.scalar.copy(by_plane[:, t, lo:hi], windows[t][:, lo:hi])
 
         last = PACK - 1
-        for lo, hi in SCALAR_LAST:
+        for lo, hi in SCALAR_LAST_EARLY:
             nc.scalar.copy(by_plane[:, last, lo:hi], windows[last][:, lo:hi])
-        for lo, hi in VECTOR_LAST:
+        for k in range(pair_pieces):
+            lo = pair_lo + k * PIECE
+            nc.scalar.copy(pair_planes[:, 1, 1, k], windows[last][:, lo : lo + PIECE])
+        for lo, hi in SCALAR_LAST_LATE:
+            nc.scalar.copy(by_plane[:, last, lo:hi], windows[last][:, lo:hi])
+        for lo, hi in VECTOR_LAST[:2]:
             nc.vector.tensor_copy(by_plane[:, last, lo:hi], windows[last][:, lo:hi])
-        quantise_group(0)
+        quantise_and_store(*WORD_STORES[0])
+        for lo, hi in VECTOR_LAST[2:]:
+            nc.vector.tensor_copy(by_plane[:, last, lo:hi], windows[last][:, lo:hi])
         for k in range(pair_pieces):
             lo = pair_lo + k * PIECE
             nc.vector.tensor_copy(
                 grouped[:, PACK * lo : PACK * (lo + PIECE)].bitcast(I32).rearrange("p (c h) -> p c h", h=2),
                 pair_values[:, k],
             )
-        for g in range(1, U // GROUP):
-            quantise_group(g)
+        for first, end in WORD_STORES[1:]:
+            quantise_and_store(first, end)
 
         scale_out = out_2[0].bitcast(I32).rearrange("(q r) (g c) -> q g r c", r=4, g=U // GROUP)
         for q in range(4):

@@ -43,7 +43,6 @@ def tile_picked_phput_none_po_kernel(tc, x_words, x_scales, mem, w1, offs, slot,
         scale_table = keep.tile([P, T], U8, name="scale_table", tag="room0", align_bytes=64)
         x_scale = keep.tile([P, S], U8, name="x_scale", align_bytes=64)
         nc.vector.memset(scale_table[:].bitcast(I32), 0)
-        nc.vector.memset(x_scale[:].bitcast(I32), 0)
 
         w_raw = keep.tile([P, PACK, N], F32, name="w_raw", tag="room1", align_bytes=64)
         w_rows = w1.rearrange("(p j) n -> p j n", j=PACK)
@@ -51,15 +50,18 @@ def tile_picked_phput_none_po_kernel(tc, x_words, x_scales, mem, w1, offs, slot,
         word_rows = x_words[0].rearrange("p c r -> p (c r)").bitcast(I32)
         nc.sync.dma_start(w_raw[:, 0:1, :], w_rows[:, 0:1, :])
         nc.sync.dma_start(offs_sb[:], offs)
-        nc.sync.dma_start(scale_table[0:P:8, :].bitcast(I32), x_scales[0].bitcast(I32))
+        scale_rows = x_scales[0].bitcast(I32).rearrange("(g v) c -> v g c", v=2)
+        for v in range(2):
+            nc.sync.dma_start(scale_table[v:P:16, :].bitcast(I32), scale_rows[v])
         nc.sync.dma_start(w_raw[:, 1:PACK, :], w_rows[:, 1:PACK, :])
         nc.sync.dma_start(word_table[:].bitcast(I32), word_rows)
         nc.sync.dma_start(slot_sb[:], slot)
 
         picked_scale = keep.tile([P, S], U8, name="picked_scale", align_bytes=64)
         nc.vector.tensor_copy(picked_scale[:], scale_table[:].indirect(offs_sb[:]))
-        for q in range(4):
-            nc.sync.dma_start(x_scale[32 * q : 32 * q + 4, :].bitcast(I32), picked_scale[32 * q : 32 * q + 32 : 8, :].bitcast(I32))
+        nc.vector.tensor_copy(x_scale[:].bitcast(I32), picked_scale[:].bitcast(I32))
+        for v in range(2):
+            nc.sync.dma_start(x_scale[2 + v : P : 32, :].bitcast(I32), picked_scale[16 + v : P : 32, :].bitcast(I32))
 
         w_bf = keep.tile([P, PACK * N], BF16, name="w_bf", tag="room2", align_bytes=64)
         w_dealt = w_bf[:].rearrange("p (t m j) -> p m t j", t=PACK, j=PACK)

@@ -44,7 +44,7 @@ def tile_picked_phput_none_po_kernel(tc, x_words, x_scales, mem, w1, offs, slot,
         x_scale = keep.tile([P, S], U8, name="x_scale", align_bytes=64)
         nc.vector.memset(scale_table[:].bitcast(I32), 0)
 
-        w_raw = keep.tile([P, PACK, N], F32, name="w_raw", tag="room1", align_bytes=64)
+        w_raw = keep.tile([P, PACK, N], F32, name="w_raw", align_bytes=64)
         w_rows = w1.rearrange("(p j) n -> p j n", j=PACK)
         word_table = keep.tile([P, T], U32, name="word_table", tag="room3", align_bytes=64)
         word_rows = x_words[0].rearrange("p c r -> p (c r)").bitcast(I32)
@@ -57,22 +57,28 @@ def tile_picked_phput_none_po_kernel(tc, x_words, x_scales, mem, w1, offs, slot,
         nc.sync.dma_start(word_table[:].bitcast(I32), word_rows)
         nc.sync.dma_start(slot_sb[:], slot)
 
-        picked_scale = keep.tile([P, S], U8, name="picked_scale", align_bytes=64)
+        picked_scale = keep.tile([P, S], U8, name="picked_scale", tag="room1", align_bytes=64)
         nc.vector.tensor_copy(picked_scale[:], scale_table[:].indirect(offs_sb[:]))
         nc.vector.tensor_copy(x_scale[:].bitcast(I32), picked_scale[:].bitcast(I32))
         for v in range(2):
             nc.sync.dma_start(x_scale[2 + v : P : 32, :].bitcast(I32), picked_scale[16 + v : P : 32, :].bitcast(I32))
 
-        w_bf = keep.tile([P, PACK * N], BF16, name="w_bf", tag="room2", align_bytes=64)
-        w_dealt = w_bf[:].rearrange("p (t m j) -> p m t j", t=PACK, j=PACK)
-        nc.vector.tensor_copy(w_dealt, w_raw[:].rearrange("p j (m t) -> p m t j", t=PACK))
         w_codes = keep.tile([P, N], U32, name="w_codes", align_bytes=64)
         w_scale = keep.tile([P, N], U8, name="w_scale", align_bytes=64)
-        nc.vector.quantize_mx(out=w_codes[:].bitcast(FP8X4), scales=w_scale[:], in_=w_bf[:])
+        w_by_plane = w_raw[:].rearrange("p j (m t) -> p m t j", t=PACK)
 
+        def quantise_weights(half, tag):
+            w_bf = keep.tile([P, 2 * N], BF16, name="w_bf%d" % half, tag=tag, align_bytes=64)
+            w_dealt = w_bf[:].rearrange("p (t m j) -> p m t j", t=2, j=PACK)
+            nc.vector.tensor_copy(w_dealt, w_by_plane[:, :, 2 * half : 2 * half + 2, :])
+            cols = slice(2 * P * half, 2 * P * (half + 1))
+            nc.vector.quantize_mx(out=w_codes[:, cols].bitcast(FP8X4), scales=w_scale[:, cols], in_=w_bf[:])
+
+        quantise_weights(0, "room2")
         x_codes = keep.tile([P, S], U32, name="x_codes", align_bytes=64)
         for lo in (0, HALF):
             nc.vector.tensor_copy(x_codes[:, lo : lo + HALF], word_table[:].indirect(offs_sb[:, lo // 16 : (lo + HALF) // 16]))
+        quantise_weights(1, "room3")
 
         mem_rows = mem.rearrange("(p t) c -> t p c", t=PACK)
         out_rows = out_0.rearrange("(p t) c -> t p c", t=PACK)

@@ -63,22 +63,21 @@ def tile_picked_phput_none_po_kernel(tc, x_words, x_scales, mem, w1, offs, slot,
         for v in range(2):
             nc.sync.dma_start(x_scale[2 + v : P : 32, :].bitcast(I32), picked_scale[16 + v : P : 32, :].bitcast(I32))
 
-        w_codes = keep.tile([P, N], U32, name="w_codes", align_bytes=64)
         w_scale = keep.tile([P, N], U8, name="w_scale", align_bytes=64)
         w_by_plane = w_raw[:].rearrange("p j (m t) -> p m t j", t=PACK)
 
-        def quantise_weights(half, tag):
-            w_bf = keep.tile([P, 2 * N], BF16, name="w_bf%d" % half, tag=tag, align_bytes=64)
-            w_dealt = w_bf[:].rearrange("p (t m j) -> p m t j", t=2, j=PACK)
-            nc.vector.tensor_copy(w_dealt, w_by_plane[:, :, 2 * half : 2 * half + 2, :])
-            cols = slice(2 * P * half, 2 * P * (half + 1))
-            nc.vector.quantize_mx(out=w_codes[:, cols].bitcast(FP8X4), scales=w_scale[:, cols], in_=w_bf[:])
-
-        quantise_weights(0, "room2")
+        w_bf0 = keep.tile([P, 2 * N], BF16, name="w_bf0", tag="room2", align_bytes=64)
+        w_bf1 = keep.tile([P, 2 * N], BF16, name="w_bf1", align_bytes=64)
+        nc.vector.tensor_copy(w_bf0[:].rearrange("p (t m j) -> p m t j", t=2, j=PACK), w_by_plane[:, :, 0:2, :])
+        nc.scalar.copy(w_bf1[:].rearrange("p (t m j) -> p m t j", t=2, j=PACK), w_by_plane[:, :, 2:4, :])
+        w_codes0 = keep.tile([P, 2 * P], U32, name="w_codes0", align_bytes=64)
+        nc.vector.quantize_mx(out=w_codes0[:].bitcast(FP8X4), scales=w_scale[:, 0 : 2 * P], in_=w_bf0[:])
         x_codes = keep.tile([P, S], U32, name="x_codes", align_bytes=64)
         for lo in (0, HALF):
             nc.vector.tensor_copy(x_codes[:, lo : lo + HALF], word_table[:].indirect(offs_sb[:, lo // 16 : (lo + HALF) // 16]))
-        quantise_weights(1, "room3")
+        w_codes1 = keep.tile([P, 2 * P], U32, name="w_codes1", tag="room3", align_bytes=64)
+        nc.vector.quantize_mx(out=w_codes1[:].bitcast(FP8X4), scales=w_scale[:, 2 * P : N], in_=w_bf1[:])
+        w_codes = (w_codes0, w_codes1)
 
         mem_rows = mem.rearrange("(p t) c -> t p c", t=PACK)
         out_rows = out_0.rearrange("(p t) c -> t p c", t=PACK)
@@ -96,7 +95,7 @@ def tile_picked_phput_none_po_kernel(tc, x_words, x_scales, mem, w1, offs, slot,
                 acc = psum.tile([P, hi - lo], F32, name="acc%d_%d" % (t, lo))
                 nc.tensor.matmul_mx(
                     out=acc[:],
-                    lhsT=w_codes[:, cols].bitcast(FP8X4),
+                    lhsT=w_codes[t // 2][:, t % 2 * P : (t % 2 + 1) * P].bitcast(FP8X4),
                     lhsT_scale=w_scale[:, cols],
                     rhs=x_codes[:, lo:hi].bitcast(FP8X4),
                     rhs_scale=x_scale[:, lo:hi],

@@ -18,21 +18,14 @@ PACK = 4
 HALF = S // 2
 PIECE = 256
 GROUP = 512
-
-FIRST_PASSES = ((0, HALF), (HALF, HALF + P), (HALF + P, S))
-
-GPSIMD_IN_PLACE = ((0, 512), (1536, 1920))
-SCALAR_PAIRS = (1024, 1536)
-SCALAR_IN_PLACE = ((512, 1024), (1920, 2048))
-
-VECTOR_LAST = ((0, 256), (256, 512), (1536, 1664))
-SCALAR_LAST_EARLY = ((512, 768), (768, 1024))
-SCALAR_LAST_LATE = ((1664, 1792), (1792, 2048))
+GROUPS = U // GROUP
 WORD_STORES = ((0, 1024), (1024, 1536), (1536, 2048))
 
 
 def tile_picked_phput_none_po_kernel(tc, x_words, x_scales, mem, w1, offs, slot, out_0, out_1, out_2):
     nc = tc.nc
+    copy = mybir.ActivationFunctionType.Copy
+    mult, add = mybir.AluOpType.mult, mybir.AluOpType.add
     with ExitStack() as ctx:
         lists = ctx.enter_context(tc.tile_pool(name="lists", bufs=1))
         keep = ctx.enter_context(tc.tile_pool(name="keep", bufs=1))
@@ -46,7 +39,7 @@ def tile_picked_phput_none_po_kernel(tc, x_words, x_scales, mem, w1, offs, slot,
 
         w_raw = keep.tile([P, PACK, N], F32, name="w_raw", align_bytes=64)
         w_rows = w1.rearrange("(p j) n -> p j n", j=PACK)
-        word_table = keep.tile([P, T], U32, name="word_table", tag="room3", align_bytes=64)
+        word_table = keep.tile([P, T], U32, name="word_table", tag="room2", align_bytes=64)
         word_rows = x_words[0].rearrange("p c r -> p (c r)").bitcast(I32)
         nc.sync.dma_start(w_raw[:, 0:1, :], w_rows[:, 0:1, :])
         nc.sync.dma_start(offs_sb[:], offs)
@@ -57,7 +50,10 @@ def tile_picked_phput_none_po_kernel(tc, x_words, x_scales, mem, w1, offs, slot,
         nc.sync.dma_start(word_table[:].bitcast(I32), word_rows)
         nc.sync.dma_start(slot_sb[:], slot)
 
-        picked_scale = keep.tile([P, S], U8, name="picked_scale", tag="room1", align_bytes=64)
+        mem_rows = mem.rearrange("(p t) c -> t p c", t=PACK)
+        out_rows = out_0.rearrange("(p t) c -> t p c", t=PACK)
+
+        picked_scale = keep.tile([P, S], U8, name="picked_scale", tag="room3", align_bytes=64)
         nc.vector.tensor_copy(picked_scale[:], scale_table[:].indirect(offs_sb[:]))
         nc.vector.tensor_copy(x_scale[:].bitcast(I32), picked_scale[:].bitcast(I32))
         for v in range(2):
@@ -65,33 +61,34 @@ def tile_picked_phput_none_po_kernel(tc, x_words, x_scales, mem, w1, offs, slot,
 
         w_scale = keep.tile([P, N], U8, name="w_scale", align_bytes=64)
         w_by_plane = w_raw[:].rearrange("p j (m t) -> p m t j", t=PACK)
-
-        w_bf0 = keep.tile([P, 2 * N], BF16, name="w_bf0", tag="room2", align_bytes=64)
+        w_bf0 = keep.tile([P, 2 * N], BF16, name="w_bf0", tag="room1", align_bytes=64)
         w_bf1 = keep.tile([P, 2 * N], BF16, name="w_bf1", align_bytes=64)
         nc.vector.tensor_copy(w_bf0[:].rearrange("p (t m j) -> p m t j", t=2, j=PACK), w_by_plane[:, :, 0:2, :])
-        nc.scalar.copy(w_bf1[:].rearrange("p (t m j) -> p m t j", t=2, j=PACK), w_by_plane[:, :, 2:4, :])
+        nc.scalar.activation(w_bf1[:].rearrange("p (t m j) -> p m t j", t=2, j=PACK), w_by_plane[:, :, 2:4, :], copy)
         w_codes0 = keep.tile([P, 2 * P], U32, name="w_codes0", align_bytes=64)
         nc.vector.quantize_mx(out=w_codes0[:].bitcast(FP8X4), scales=w_scale[:, 0 : 2 * P], in_=w_bf0[:])
         x_codes = keep.tile([P, S], U32, name="x_codes", align_bytes=64)
         for lo in (0, HALF):
             nc.vector.tensor_copy(x_codes[:, lo : lo + HALF], word_table[:].indirect(offs_sb[:, lo // 16 : (lo + HALF) // 16]))
-        w_codes1 = keep.tile([P, 2 * P], U32, name="w_codes1", tag="room3", align_bytes=64)
+        w_codes1 = keep.tile([P, 2 * P], U32, name="w_codes1", align_bytes=64)
         nc.vector.quantize_mx(out=w_codes1[:].bitcast(FP8X4), scales=w_scale[:, 2 * P : N], in_=w_bf1[:])
         w_codes = (w_codes0, w_codes1)
 
-        mem_rows = mem.rearrange("(p t) c -> t p c", t=PACK)
-        out_rows = out_0.rearrange("(p t) c -> t p c", t=PACK)
         windows = []
         for t in range(PACK):
             window = keep.tile([P, U], F32, name="window%d" % t, tag="room%d" % t, align_bytes=64)
             nc.sync.dma_start(window[:], mem_rows[t])
             windows.append(window)
 
-        ys = []
+        pairs = [keep.tile([P, PACK * GROUP], BF16, name="pairs%d" % g, align_bytes=64) for g in range(GROUPS)]
+        ys = {}
         for t in range(PACK):
-            y = keep.tile([P, S], F32, name="y%d" % t)
+            if t == 3:
+                y = pairs[0][:, 2 * GROUP : PACK * GROUP].bitcast(F32)
+            else:
+                y = keep.tile([P, S], F32, name="y%d" % t)
             cols = slice(t * P, (t + 1) * P)
-            for lo, hi in FIRST_PASSES if t == 0 else ((0, S),):
+            for lo, hi in ((0, HALF), (HALF, S)) if t == 0 else ((0, S),):
                 acc = psum.tile([P, hi - lo], F32, name="acc%d_%d" % (t, lo))
                 nc.tensor.matmul_mx(
                     out=acc[:],
@@ -102,67 +99,64 @@ def tile_picked_phput_none_po_kernel(tc, x_words, x_scales, mem, w1, offs, slot,
                     start=True,
                     stop=True,
                 )
-                nc.scalar.copy(y[:, lo:hi], acc[:])
-            ys.append(y)
+                if (t, lo) == (0, 0):
+                    nc.scalar.copy(y[:, lo:hi], acc[:])
+                else:
+                    nc.vector.tensor_copy(y[:, lo:hi], acc[:])
+            ys[t] = y
 
-        pair_lo, pair_hi = SCALAR_PAIRS
-        pair_pieces = (pair_hi - pair_lo) // PIECE
-        grouped = keep.tile([P, PACK * U], BF16, name="grouped", align_bytes=64)
-        by_plane = grouped[:].rearrange("p (c t) -> p t c", t=PACK)
-        by_column = grouped[:].rearrange("p (c t) -> p c t", t=PACK)
-        pairs = keep.tile([P, PACK * (pair_hi - pair_lo)], BF16, name="pairs", align_bytes=64)
-        pair_planes = pairs[:].rearrange("p (k h c e) -> p h e k c", k=pair_pieces, h=2, e=2)
-        pair_values = pairs[:].bitcast(I32).rearrange("p (k h c) -> p k c h", k=pair_pieces, h=2)
+        grouped = [keep.tile([P, PACK * GROUP], BF16, name="grouped%d" % g, align_bytes=64) for g in range(GROUPS)]
         out_scale = keep.tile([P, GROUP], U8, name="out_scale", align_bytes=64)
         codes = keep.tile([P, U], U32, name="codes", align_bytes=64)
         out_words = out_1[0].rearrange("p c r -> p (c r)").bitcast(I32)
-        mult, add = mybir.AluOpType.mult, mybir.AluOpType.add
 
-        def quantise_and_store(first, end):
-            for lo in range(first, end, PIECE):
+        def pair_place(g, t):
+            return pairs[g][:].rearrange("p (h c e) -> p h e c", h=2, e=2)[:, t // 2, t % 2]
+
+        def columns(g, t):
+            return windows[t][:, g * GROUP : (g + 1) * GROUP]
+
+        def weave(g, engine):
+            if engine == "vector":
+                nc.vector.tensor_copy(grouped[g][:].bitcast(I32).rearrange("p (c h) -> p c h", h=2), pairs[g][:].bitcast(I32).rearrange("p (h c) -> p c h", h=2))
+            else:
+                nc.scalar.copy(grouped[g][:].bitcast(U32).rearrange("p (c h) -> p c h", h=2), pairs[g][:].bitcast(U32).rearrange("p (h c) -> p c h", h=2))
+
+        def quantise(g):
+            for lo in range(0, GROUP, PIECE):
                 nc.vector.quantize_mx(
-                    out=codes[:, lo : lo + PIECE].bitcast(FP8X4),
-                    scales=out_scale[4 * (lo // GROUP) : P, lo % GROUP : lo % GROUP + PIECE],
-                    in_=grouped[:, PACK * lo : PACK * (lo + PIECE)],
+                    out=codes[:, g * GROUP + lo : g * GROUP + lo + PIECE].bitcast(FP8X4),
+                    scales=out_scale[4 * g : P, lo : lo + PIECE],
+                    in_=grouped[g][:, PACK * lo : PACK * (lo + PIECE)],
                 )
-            nc.sync.dma_start(out_words[:, first:end], codes[:, first:end].bitcast(I32))
 
         for t in range(PACK):
-            nc.vector.tensor_copy(windows[t][:].indirect(slot_sb[:]), ys[t][:])
+            if t % 2 == 0:
+                for lo in (0, HALF):
+                    nc.scalar.activation(windows[t][:].indirect(slot_sb[:, lo // 16 : (lo + HALF) // 16]), ys[t][:, lo : lo + HALF], copy)
+            else:
+                nc.vector.tensor_copy(windows[t][:].indirect(slot_sb[:]), ys[t][:, 0:S])
             nc.sync.dma_start(out_rows[t], windows[t][:])
-            for lo, hi in GPSIMD_IN_PLACE:
-                if t < 2:
-                    nc.gpsimd.tensor_scalar(by_plane[:, t, lo:hi], windows[t][:, lo:hi], 1.0, -0.0, mult, add)
-                elif t == 2:
-                    twice = windows[t][:, lo:hi].unsqueeze(2).to_broadcast([P, hi - lo, 2])
-                    nc.gpsimd.tensor_scalar(by_column[:, lo:hi, 2:4], twice, 1.0, -0.0, mult, add)
-            if t < PACK - 1:
-                nc.scalar.copy(pair_planes[:, t // 2, t % 2], windows[t][:, pair_lo:pair_hi].rearrange("p (k c) -> p k c", k=pair_pieces))
-                for lo, hi in SCALAR_IN_PLACE:
-                    nc.scalar.copy(by_plane[:, t, lo:hi], windows[t][:, lo:hi])
 
-        last = PACK - 1
-        for lo, hi in SCALAR_LAST_EARLY:
-            nc.scalar.copy(by_plane[:, last, lo:hi], windows[last][:, lo:hi])
-        for k in range(pair_pieces):
-            lo = pair_lo + k * PIECE
-            nc.scalar.copy(pair_planes[:, 1, 1, k], windows[last][:, lo : lo + PIECE])
-        for lo, hi in SCALAR_LAST_LATE:
-            nc.scalar.copy(by_plane[:, last, lo:hi], windows[last][:, lo:hi])
-        for lo, hi in VECTOR_LAST[:2]:
-            nc.vector.tensor_copy(by_plane[:, last, lo:hi], windows[last][:, lo:hi])
-        quantise_and_store(*WORD_STORES[0])
-        for lo, hi in VECTOR_LAST[2:]:
-            nc.vector.tensor_copy(by_plane[:, last, lo:hi], windows[last][:, lo:hi])
-        for k in range(pair_pieces):
-            lo = pair_lo + k * PIECE
-            nc.vector.tensor_copy(
-                grouped[:, PACK * lo : PACK * (lo + PIECE)].bitcast(I32).rearrange("p (c h) -> p c h", h=2),
-                pair_values[:, k],
-            )
-        for first, end in WORD_STORES[1:]:
-            quantise_and_store(first, end)
+        for t in (0, 1):
+            for g in range(GROUPS):
+                nc.gpsimd.tensor_scalar(pair_place(g, t), columns(g, t), 1.0, -0.0, mult, add)
+        for t in (2, 3):
+            nc.vector.tensor_copy(pair_place(0, t), columns(0, t))
+            for g in range(1, GROUPS):
+                nc.scalar.copy(pair_place(g, t), columns(g, t))
 
-        scale_out = out_2[0].bitcast(I32).rearrange("(q r) (g c) -> q g r c", r=4, g=U // GROUP)
+        weave(0, "vector")
+        weave(1, "vector")
+        quantise(0)
+        weave(2, "vector")
+        quantise(1)
+        weave(3, "scalar")
+        quantise(2)
+        quantise(3)
+        for first, end in WORD_STORES:
+            nc.sync.dma_start(out_words[:, first:end], codes[:, first:end].bitcast(I32))
+
+        scale_out = out_2[0].bitcast(I32).rearrange("(q r) (g c) -> q g r c", r=4, g=GROUPS)
         for q in range(4):
             nc.sync.dma_start(scale_out[q], out_scale[32 * q : 32 * q + 16, :].bitcast(I32))

@@ -20,6 +20,12 @@ PIECE = 256
 GROUP = 512
 GROUPS = U // GROUP
 WORD_STORES = ((0, 1024), (1024, 1536), (1536, 2048))
+GPSIMD_LOW = ((0, 512), (512, 1024), (1024, 1536))
+SCALAR_LOW = ((1536, 2048),)
+VECTOR_HIGH = ((0, 512), (512, 1024), (1024, 1536))
+SCALAR_HIGH = ((1536, 2048),)
+VECTOR_WEAVES = ((0, 512), (512, 1024))
+SCALAR_WEAVES = ((1024, 1536), (1536, 2048))
 
 
 def tile_picked_phput_none_po_kernel(tc, x_words, x_scales, mem, w1, offs, slot, out_0, out_1, out_2):
@@ -39,7 +45,7 @@ def tile_picked_phput_none_po_kernel(tc, x_words, x_scales, mem, w1, offs, slot,
 
         w_raw = keep.tile([P, PACK, N], F32, name="w_raw", align_bytes=64)
         w_rows = w1.rearrange("(p j) n -> p j n", j=PACK)
-        word_table = keep.tile([P, T], U32, name="word_table", tag="room2", align_bytes=64)
+        word_table = keep.tile([P, T], U32, name="word_table", tag="room3", align_bytes=64)
         word_rows = x_words[0].rearrange("p c r -> p (c r)").bitcast(I32)
         nc.sync.dma_start(w_raw[:, 0:1, :], w_rows[:, 0:1, :])
         nc.sync.dma_start(offs_sb[:], offs)
@@ -53,18 +59,18 @@ def tile_picked_phput_none_po_kernel(tc, x_words, x_scales, mem, w1, offs, slot,
         mem_rows = mem.rearrange("(p t) c -> t p c", t=PACK)
         out_rows = out_0.rearrange("(p t) c -> t p c", t=PACK)
 
-        picked_scale = keep.tile([P, S], U8, name="picked_scale", tag="room3", align_bytes=64)
+        picked_scale = keep.tile([P, S], U8, name="picked_scale", tag="room2", align_bytes=64)
         nc.vector.tensor_copy(picked_scale[:], scale_table[:].indirect(offs_sb[:]))
         nc.vector.tensor_copy(x_scale[:].bitcast(I32), picked_scale[:].bitcast(I32))
         for v in range(2):
             nc.sync.dma_start(x_scale[2 + v : P : 32, :].bitcast(I32), picked_scale[16 + v : P : 32, :].bitcast(I32))
 
         w_scale = keep.tile([P, N], U8, name="w_scale", align_bytes=64)
-        w_by_plane = w_raw[:].rearrange("p j (m t) -> p m t j", t=PACK)
+        w_by_plane = w_raw[:].rearrange("p j (m h e) -> p h m e j", h=2, e=2)
         w_bf0 = keep.tile([P, 2 * N], BF16, name="w_bf0", tag="room1", align_bytes=64)
         w_bf1 = keep.tile([P, 2 * N], BF16, name="w_bf1", align_bytes=64)
-        nc.vector.tensor_copy(w_bf0[:].rearrange("p (t m j) -> p m t j", t=2, j=PACK), w_by_plane[:, :, 0:2, :])
-        nc.scalar.activation(w_bf1[:].rearrange("p (t m j) -> p m t j", t=2, j=PACK), w_by_plane[:, :, 2:4, :], copy)
+        nc.vector.tensor_copy(w_bf0[:].rearrange("p (e m j) -> p m e j", e=2, j=PACK), w_by_plane[:, 0])
+        nc.scalar.activation(w_bf1[:].rearrange("p (e m j) -> p m e j", e=2, j=PACK), w_by_plane[:, 1], copy)
         w_codes0 = keep.tile([P, 2 * P], U32, name="w_codes0", align_bytes=64)
         nc.vector.quantize_mx(out=w_codes0[:].bitcast(FP8X4), scales=w_scale[:, 0 : 2 * P], in_=w_bf0[:])
         x_codes = keep.tile([P, S], U32, name="x_codes", align_bytes=64)
@@ -74,26 +80,31 @@ def tile_picked_phput_none_po_kernel(tc, x_words, x_scales, mem, w1, offs, slot,
         nc.vector.quantize_mx(out=w_codes1[:].bitcast(FP8X4), scales=w_scale[:, 2 * P : N], in_=w_bf1[:])
         w_codes = (w_codes0, w_codes1)
 
-        windows = []
-        for t in range(PACK):
-            window = keep.tile([P, U], F32, name="window%d" % t, tag="room%d" % t, align_bytes=64)
-            nc.sync.dma_start(window[:], mem_rows[t])
-            windows.append(window)
+        order = (0, 1, 2, 3)
+        windows = {}
+        for room, t in enumerate(order):
+            windows[t] = keep.tile([P, U], F32, name="window%d" % t, tag="room%d" % room, align_bytes=64)
+            nc.sync.dma_start(windows[t][:], mem_rows[t])
 
         pairs = [keep.tile([P, PACK * GROUP], BF16, name="pairs%d" % g, align_bytes=64) for g in range(GROUPS)]
+
+        def place(t, lo, hi):
+            g = lo // GROUP
+            return pairs[g][:].rearrange("p (h c e) -> p h e c", h=2, e=2)[:, t // 2, t % 2, lo - g * GROUP : hi - g * GROUP]
+
         ys = {}
-        for t in range(PACK):
+        for t in (0, 2, 3, 1):
             if t == 3:
-                y = pairs[0][:, 2 * GROUP : PACK * GROUP].bitcast(F32)
+                y = pairs[GROUPS - 1][:, 2 * GROUP : PACK * GROUP].bitcast(F32)
             else:
                 y = keep.tile([P, S], F32, name="y%d" % t)
-            cols = slice(t * P, (t + 1) * P)
+            e, h = t % 2, t // 2
             for lo, hi in ((0, HALF), (HALF, S)) if t == 0 else ((0, S),):
                 acc = psum.tile([P, hi - lo], F32, name="acc%d_%d" % (t, lo))
                 nc.tensor.matmul_mx(
                     out=acc[:],
-                    lhsT=w_codes[t // 2][:, t % 2 * P : (t % 2 + 1) * P].bitcast(FP8X4),
-                    lhsT_scale=w_scale[:, cols],
+                    lhsT=w_codes[h][:, e * P : (e + 1) * P].bitcast(FP8X4),
+                    lhsT_scale=w_scale[:, t * P : (t + 1) * P],
                     rhs=x_codes[:, lo:hi].bitcast(FP8X4),
                     rhs_scale=x_scale[:, lo:hi],
                     start=True,
@@ -106,55 +117,46 @@ def tile_picked_phput_none_po_kernel(tc, x_words, x_scales, mem, w1, offs, slot,
             ys[t] = y
 
         grouped = [keep.tile([P, PACK * GROUP], BF16, name="grouped%d" % g, align_bytes=64) for g in range(GROUPS)]
+
+        def weave_views(lo, hi, dtype):
+            g = lo // GROUP
+            cols = slice(lo - g * GROUP, hi - g * GROUP)
+            return grouped[g][:].bitcast(dtype).rearrange("p (c h) -> p c h", h=2)[:, cols], pairs[g][:].bitcast(dtype).rearrange("p (h c) -> p c h", h=2)[:, cols]
+
         out_scale = keep.tile([P, GROUP], U8, name="out_scale", align_bytes=64)
         codes = keep.tile([P, U], U32, name="codes", align_bytes=64)
         out_words = out_1[0].rearrange("p c r -> p (c r)").bitcast(I32)
 
-        def pair_place(g, t):
-            return pairs[g][:].rearrange("p (h c e) -> p h e c", h=2, e=2)[:, t // 2, t % 2]
-
-        def columns(g, t):
-            return windows[t][:, g * GROUP : (g + 1) * GROUP]
-
-        def weave(g, engine):
-            if engine == "vector":
-                nc.vector.tensor_copy(grouped[g][:].bitcast(I32).rearrange("p (c h) -> p c h", h=2), pairs[g][:].bitcast(I32).rearrange("p (h c) -> p c h", h=2))
-            else:
-                nc.scalar.copy(grouped[g][:].bitcast(U32).rearrange("p (c h) -> p c h", h=2), pairs[g][:].bitcast(U32).rearrange("p (h c) -> p c h", h=2))
-
-        def quantise(g):
-            for lo in range(0, GROUP, PIECE):
-                nc.vector.quantize_mx(
-                    out=codes[:, g * GROUP + lo : g * GROUP + lo + PIECE].bitcast(FP8X4),
-                    scales=out_scale[4 * g : P, lo : lo + PIECE],
-                    in_=grouped[g][:, PACK * lo : PACK * (lo + PIECE)],
-                )
-
-        for t in range(PACK):
-            if t % 2 == 0:
+        for t in order:
+            if t in (0, 3):
                 for lo in (0, HALF):
                     nc.scalar.activation(windows[t][:].indirect(slot_sb[:, lo // 16 : (lo + HALF) // 16]), ys[t][:, lo : lo + HALF], copy)
             else:
                 nc.vector.tensor_copy(windows[t][:].indirect(slot_sb[:]), ys[t][:, 0:S])
             nc.sync.dma_start(out_rows[t], windows[t][:])
-
-        for t in (0, 1):
-            for g in range(GROUPS):
-                nc.gpsimd.tensor_scalar(pair_place(g, t), columns(g, t), 1.0, -0.0, mult, add)
+            if t < 2:
+                for lo, hi in SCALAR_LOW:
+                    nc.scalar.copy(place(t, lo, hi), windows[t][:, lo:hi])
+                for lo, hi in GPSIMD_LOW:
+                    nc.gpsimd.tensor_scalar(place(t, lo, hi), windows[t][:, lo:hi], 1.0, -0.0, mult, add)
+            else:
+                for lo, hi in VECTOR_HIGH:
+                    nc.vector.tensor_copy(place(t, lo, hi), windows[t][:, lo:hi])
         for t in (2, 3):
-            nc.vector.tensor_copy(pair_place(0, t), columns(0, t))
-            for g in range(1, GROUPS):
-                nc.scalar.copy(pair_place(g, t), columns(g, t))
+            for lo, hi in SCALAR_HIGH:
+                nc.scalar.copy(place(t, lo, hi), windows[t][:, lo:hi])
 
-        weave(0, "vector")
-        weave(1, "vector")
-        quantise(0)
-        weave(2, "vector")
-        quantise(1)
-        weave(3, "scalar")
-        quantise(2)
-        quantise(3)
+        for lo, hi in VECTOR_WEAVES:
+            nc.vector.tensor_copy(*weave_views(lo, hi, I32))
+        for lo, hi in SCALAR_WEAVES:
+            nc.scalar.copy(*weave_views(lo, hi, U32))
         for first, end in WORD_STORES:
+            for lo in range(first, end, PIECE):
+                nc.vector.quantize_mx(
+                    out=codes[:, lo : lo + PIECE].bitcast(FP8X4),
+                    scales=out_scale[4 * (lo // GROUP) : P, lo % GROUP : lo % GROUP + PIECE],
+                    in_=grouped[lo // GROUP][:, PACK * (lo % GROUP) : PACK * (lo % GROUP + PIECE)],
+                )
             nc.sync.dma_start(out_words[:, first:end], codes[:, first:end].bitcast(I32))
 
         scale_out = out_2[0].bitcast(I32).rearrange("(q r) (g c) -> q g r c", r=4, g=GROUPS)

@@ -70,7 +70,8 @@ def tile_picked_phput_none_po_kernel(tc, x_words, x_scales, mem, w1, offs, slot,
         w_bf0 = keep.tile([P, 2 * N], BF16, name="w_bf0", tag="room1", align_bytes=64)
         w_bf1 = keep.tile([P, 2 * N], BF16, name="w_bf1", align_bytes=64)
         nc.vector.tensor_copy(w_bf0[:].rearrange("p (e m j) -> p m e j", e=2, j=PACK), w_by_plane[:, 0])
-        nc.scalar.activation(w_bf1[:].rearrange("p (e m j) -> p m e j", e=2, j=PACK), w_by_plane[:, 1], copy)
+        for rows in (slice(0, 1), slice(1, PACK)):
+            nc.scalar.activation(w_bf1[:].rearrange("p (e m j) -> p m e j", e=2, j=PACK)[:, :, :, rows], w_by_plane[:, 1, :, :, rows], copy)
         w_codes0 = keep.tile([P, 2 * P], U32, name="w_codes0", align_bytes=64)
         nc.vector.quantize_mx(out=w_codes0[:].bitcast(FP8X4), scales=w_scale[:, 0 : 2 * P], in_=w_bf0[:])
         x_codes = keep.tile([P, S], U32, name="x_codes", align_bytes=64)

@@ -20,9 +20,10 @@ PIECE = 256
 GROUP = 512
 GROUPS = U // GROUP
 WORD_STORES = ((0, 1024), (1024, 1536), (1536, 2048))
-GPSIMD_LOW = ((0, 512), (512, 1024), (1024, 1536))
+GPSIMD_LOW = ((0, 1536),)
 SCALAR_LOW = ((1536, 2048),)
-VECTOR_HIGH = ((0, 512), (512, 1024), (1024, 1536))
+VECTOR_HIGH = ((0, 1024), (1024, 1536))
+SPLIT = 1536
 SCALAR_HIGH = ((1536, 2048),)
 VECTOR_WEAVES = ((0, 512), (512, 1024))
 SCALAR_WEAVES = ((1024, 1536), (1536, 2048))
@@ -87,16 +88,16 @@ def tile_picked_phput_none_po_kernel(tc, x_words, x_scales, mem, w1, offs, slot,
             windows[t] = keep.tile([P, U], F32, name="window%d" % t, tag="room%d" % room, align_bytes=64)
             nc.sync.dma_start(windows[t][:], mem_rows[t])
 
-        pairs = [keep.tile([P, PACK * GROUP], BF16, name="pairs%d" % g, align_bytes=64) for g in range(GROUPS)]
+        pairs = [keep.tile([P, PACK * width], BF16, name="pairs%d" % width, align_bytes=64) for width in (SPLIT, U - SPLIT)]
 
         def place(t, lo, hi):
-            g = lo // GROUP
-            return pairs[g][:].rearrange("p (h c e) -> p h e c", h=2, e=2)[:, t // 2, t % 2, lo - g * GROUP : hi - g * GROUP]
+            side = lo // SPLIT
+            return pairs[side][:].rearrange("p (h c e) -> p h e c", h=2, e=2)[:, t // 2, t % 2, lo - side * SPLIT : hi - side * SPLIT]
 
         ys = {}
         for t in (0, 2, 3, 1):
             if t == 3:
-                y = pairs[GROUPS - 1][:, 2 * GROUP : PACK * GROUP].bitcast(F32)
+                y = pairs[1][:, 2 * GROUP : PACK * GROUP].bitcast(F32)
             else:
                 y = keep.tile([P, S], F32, name="y%d" % t)
             e, h = t % 2, t // 2
@@ -122,7 +123,7 @@ def tile_picked_phput_none_po_kernel(tc, x_words, x_scales, mem, w1, offs, slot,
         def weave_views(lo, hi, dtype):
             g = lo // GROUP
             cols = slice(lo - g * GROUP, hi - g * GROUP)
-            return grouped[g][:].bitcast(dtype).rearrange("p (c h) -> p c h", h=2)[:, cols], pairs[g][:].bitcast(dtype).rearrange("p (h c) -> p c h", h=2)[:, cols]
+            return grouped[g][:].bitcast(dtype).rearrange("p (c h) -> p c h", h=2)[:, cols], pairs[lo // SPLIT][:].bitcast(dtype).rearrange("p (h c) -> p c h", h=2)[:, lo % SPLIT : lo % SPLIT + hi - lo]
 
         out_scale = keep.tile([P, GROUP], U8, name="out_scale", align_bytes=64)
         codes = keep.tile([P, U], U32, name="codes", align_bytes=64)

@@ -19,14 +19,13 @@ HALF = S // 2
 PIECE = 256
 GROUP = 512
 GROUPS = U // GROUP
-WORD_STORES = ((0, 1024), (1024, 1536), (1536, 2048))
+WORD_STORES = ((0, 768), (768, 1536), (1536, 2048))
 GPSIMD_LOW = ((0, 1536),)
 SCALAR_LOW = ((1536, 2048),)
-VECTOR_HIGH = ((0, 1024), (1024, 1536))
-SPLIT = 1536
+VECTOR_HIGH = ((0, 768), (768, 1536))
 SCALAR_HIGH = ((1536, 2048),)
-VECTOR_WEAVES = ((0, 512), (512, 1024))
-SCALAR_WEAVES = ((1024, 1536), (1536, 2048))
+VECTOR_WEAVES = ((0, 512), (512, 896))
+SCALAR_WEAVES = ((896, 1536), (1536, 1792), (1792, 2048))
 
 
 def tile_picked_phput_none_po_kernel(tc, x_words, x_scales, mem, w1, offs, slot, out_0, out_1, out_2):
@@ -88,16 +87,16 @@ def tile_picked_phput_none_po_kernel(tc, x_words, x_scales, mem, w1, offs, slot,
             windows[t] = keep.tile([P, U], F32, name="window%d" % t, tag="room%d" % room, align_bytes=64)
             nc.sync.dma_start(windows[t][:], mem_rows[t])
 
-        pairs = [keep.tile([P, PACK * width], BF16, name="pairs%d" % width, align_bytes=64) for width in (SPLIT, U - SPLIT)]
+        pairs_and_y = keep.tile([P, PACK * U + S], BF16, name="pairs_and_y", align_bytes=64)
+        pairs = pairs_and_y[:, 0 : PACK * U]
 
         def place(t, lo, hi):
-            side = lo // SPLIT
-            return pairs[side][:].rearrange("p (h c e) -> p h e c", h=2, e=2)[:, t // 2, t % 2, lo - side * SPLIT : hi - side * SPLIT]
+            return pairs.rearrange("p (h c e) -> p h e c", h=2, e=2)[:, t // 2, t % 2, lo:hi]
 
         ys = {}
         for t in (0, 2, 3, 1):
             if t == 3:
-                y = pairs[1][:, 2 * GROUP : PACK * GROUP].bitcast(F32)
+                y = pairs_and_y[:, PACK * U - S : PACK * U + S].bitcast(F32)
             else:
                 y = keep.tile([P, S], F32, name="y%d" % t)
             e, h = t % 2, t // 2
@@ -118,12 +117,10 @@ def tile_picked_phput_none_po_kernel(tc, x_words, x_scales, mem, w1, offs, slot,
                     nc.vector.tensor_copy(y[:, lo:hi], acc[:])
             ys[t] = y
 
-        grouped = [keep.tile([P, PACK * GROUP], BF16, name="grouped%d" % g, align_bytes=64) for g in range(GROUPS)]
+        grouped = keep.tile([P, PACK * U], BF16, name="grouped", align_bytes=64)
 
         def weave_views(lo, hi, dtype):
-            g = lo // GROUP
-            cols = slice(lo - g * GROUP, hi - g * GROUP)
-            return grouped[g][:].bitcast(dtype).rearrange("p (c h) -> p c h", h=2)[:, cols], pairs[lo // SPLIT][:].bitcast(dtype).rearrange("p (h c) -> p c h", h=2)[:, lo % SPLIT : lo % SPLIT + hi - lo]
+            return grouped[:].bitcast(dtype).rearrange("p (c h) -> p c h", h=2)[:, lo:hi], pairs.bitcast(dtype).rearrange("p (h c) -> p c h", h=2)[:, lo:hi]
 
         out_scale = keep.tile([P, GROUP], U8, name="out_scale", align_bytes=64)
         codes = keep.tile([P, U], U32, name="codes", align_bytes=64)
@@ -157,7 +154,7 @@ def tile_picked_phput_none_po_kernel(tc, x_words, x_scales, mem, w1, offs, slot,
                 nc.vector.quantize_mx(
                     out=codes[:, lo : lo + PIECE].bitcast(FP8X4),
                     scales=out_scale[4 * (lo // GROUP) : P, lo % GROUP : lo % GROUP + PIECE],
-                    in_=grouped[lo // GROUP][:, PACK * (lo % GROUP) : PACK * (lo % GROUP + PIECE)],
+                    in_=grouped[:, PACK * lo : PACK * (lo + PIECE)],
                 )
             nc.sync.dma_start(out_words[:, first:end], codes[:, first:end].bitcast(I32))
 

@@ -20,12 +20,14 @@ PIECE = 256
 GROUP = 512
 GROUPS = U // GROUP
 WORD_STORES = ((0, 768), (768, 1536), (1536, 2048))
-GPSIMD_LOW = ((0, 1536),)
-SCALAR_LOW = ((1536, 2048),)
-VECTOR_HIGH = ((0, 768), (768, 1536))
-SCALAR_HIGH = ((1536, 2048),)
-VECTOR_WEAVES = ((0, 512), (512, 896))
-SCALAR_WEAVES = ((896, 1536), (1536, 1792), (1792, 2048))
+LAP = 16
+VECTOR_LOW = 592
+GPSIMD_FIRST = 720
+GPSIMD_LOW = 1792
+SCALAR_HIGH = 192
+LAST_PLANE = ((SCALAR_HIGH, 512), (512, 1024), (1024, 2048))
+VECTOR_WEAVES = ((512, 1024),)
+SCALAR_WEAVES = ((0, 512), (1024, 1536), (1536, 1792), (1792, 2048))
 
 
 def tile_picked_phput_none_po_kernel(tc, x_words, x_scales, mem, w1, offs, slot, out_0, out_1, out_2):
@@ -87,18 +89,24 @@ def tile_picked_phput_none_po_kernel(tc, x_words, x_scales, mem, w1, offs, slot,
             windows[t] = keep.tile([P, U], F32, name="window%d" % t, tag="room%d" % room, align_bytes=64)
             nc.sync.dma_start(windows[t][:], mem_rows[t])
 
-        pairs_and_y = keep.tile([P, PACK * U + S], BF16, name="pairs_and_y", align_bytes=64)
-        pairs = pairs_and_y[:, 0 : PACK * U]
+        front = S - LAP
+        pairs_and_y = keep.tile([P, 2 * front + PACK * U], BF16, name="pairs_and_y", align_bytes=64)
+        pairs = pairs_and_y[:, 2 * front : 2 * front + PACK * U]
 
         def place(t, lo, hi):
             return pairs.rearrange("p (h c e) -> p h e c", h=2, e=2)[:, t // 2, t % 2, lo:hi]
 
-        ys = {}
-        for t in (0, 2, 3, 1):
-            if t == 3:
-                y = pairs_and_y[:, PACK * U - S : PACK * U + S].bitcast(F32)
-            else:
-                y = keep.tile([P, S], F32, name="y%d" % t)
+        y0 = keep.tile([P, S], F32, name="y0")
+        y1_end = keep.tile([P, HALF], F32, name="y1_end")
+        y2 = pairs_and_y[:, 0 : 2 * S].bitcast(F32)
+        y3_end = keep.tile([P, HALF], F32, name="y3_end")
+        halves = (
+            (y0[:, 0:HALF], y0[:, HALF:S]),
+            (pairs[:, 2 * U - S : 2 * U].bitcast(F32), y1_end[:]),
+            (y2[:, 0:HALF], y2[:, HALF:S]),
+            (pairs[:, 2 * U : 2 * U + S].bitcast(F32), y3_end[:]),
+        )
+        for t in range(PACK):
             e, h = t % 2, t // 2
             for lo, hi in ((0, HALF), (HALF, S)) if t == 0 else ((0, S),):
                 acc = psum.tile([P, hi - lo], F32, name="acc%d_%d" % (t, lo))
@@ -112,10 +120,14 @@ def tile_picked_phput_none_po_kernel(tc, x_words, x_scales, mem, w1, offs, slot,
                     stop=True,
                 )
                 if (t, lo) == (0, 0):
-                    nc.scalar.copy(y[:, lo:hi], acc[:])
+                    nc.scalar.copy(halves[t][0], acc[:])
+                elif t == 0:
+                    nc.vector.tensor_copy(halves[t][1], acc[:])
+                elif t == 2:
+                    nc.vector.tensor_copy(y2, acc[:])
                 else:
-                    nc.vector.tensor_copy(y[:, lo:hi], acc[:])
-            ys[t] = y
+                    nc.vector.tensor_copy(halves[t][0], acc[:, 0:HALF])
+                    nc.vector.tensor_copy(halves[t][1], acc[:, HALF:S])
 
         grouped = keep.tile([P, PACK * U], BF16, name="grouped", align_bytes=64)
 
@@ -126,24 +138,35 @@ def tile_picked_phput_none_po_kernel(tc, x_words, x_scales, mem, w1, offs, slot,
         codes = keep.tile([P, U], U32, name="codes", align_bytes=64)
         out_words = out_1[0].rearrange("p c r -> p (c r)").bitcast(I32)
 
-        for t in order:
-            if t in (0, 3):
-                for lo in (0, HALF):
-                    nc.scalar.activation(windows[t][:].indirect(slot_sb[:, lo // 16 : (lo + HALF) // 16]), ys[t][:, lo : lo + HALF], copy)
-            else:
-                nc.vector.tensor_copy(windows[t][:].indirect(slot_sb[:]), ys[t][:, 0:S])
-            nc.sync.dma_start(out_rows[t], windows[t][:])
-            if t < 2:
-                for lo, hi in SCALAR_LOW:
-                    nc.scalar.copy(place(t, lo, hi), windows[t][:, lo:hi])
-                for lo, hi in GPSIMD_LOW:
-                    nc.gpsimd.tensor_scalar(place(t, lo, hi), windows[t][:, lo:hi], 1.0, -0.0, mult, add)
-            else:
-                for lo, hi in VECTOR_HIGH:
-                    nc.vector.tensor_copy(place(t, lo, hi), windows[t][:, lo:hi])
+        slot_halves = (slot_sb[:, 0 : HALF // 16], slot_sb[:, HALF // 16 : S // 16])
+
+        nc.scalar.activation(windows[0][:].indirect(slot_halves[0]), halves[0][0], copy)
+        nc.vector.tensor_copy(windows[0][:].indirect(slot_halves[1]), halves[0][1])
+        nc.sync.dma_start(out_rows[0], windows[0][:])
+        nc.vector.tensor_copy(place(0, LAP, VECTOR_LOW), windows[0][:, LAP:VECTOR_LOW])
+        for lo, hi in ((VECTOR_LOW, GPSIMD_FIRST), (GPSIMD_FIRST, GPSIMD_LOW)):
+            nc.gpsimd.tensor_scalar(place(0, lo, hi), windows[0][:, lo:hi], 1.0, -0.0, mult, add)
+
+        for part in range(2):
+            nc.scalar.activation(windows[1][:].indirect(slot_halves[part]), halves[1][part], copy)
+        nc.sync.dma_start(out_rows[1], windows[1][:])
+        nc.gpsimd.tensor_scalar(place(1, VECTOR_LOW, GPSIMD_LOW), windows[1][:, VECTOR_LOW:GPSIMD_LOW], 1.0, -0.0, mult, add)
+        for t in range(2):
+            nc.scalar.copy(place(t, GPSIMD_LOW, U), windows[t][:, GPSIMD_LOW:U])
+
+        nc.vector.tensor_copy(windows[2][:].indirect(slot_sb[:]), y2)
+        nc.sync.dma_start(out_rows[2], windows[2][:])
+        nc.vector.tensor_copy(place(1, 0, VECTOR_LOW), windows[1][:, 0:VECTOR_LOW])
+        nc.vector.tensor_copy(place(0, 0, LAP), windows[0][:, 0:LAP])
+
+        for part in range(2):
+            nc.scalar.activation(windows[3][:].indirect(slot_halves[part]), halves[3][part], copy)
+        nc.sync.dma_start(out_rows[3], windows[3][:])
+        nc.vector.tensor_copy(place(2, SCALAR_HIGH, U), windows[2][:, SCALAR_HIGH:U])
         for t in (2, 3):
-            for lo, hi in SCALAR_HIGH:
-                nc.scalar.copy(place(t, lo, hi), windows[t][:, lo:hi])
+            nc.scalar.copy(place(t, 0, SCALAR_HIGH), windows[t][:, 0:SCALAR_HIGH])
+        for lo, hi in LAST_PLANE:
+            nc.vector.tensor_copy(place(3, lo, hi), windows[3][:, lo:hi])
 
         for lo, hi in VECTOR_WEAVES:
             nc.vector.tensor_copy(*weave_views(lo, hi, I32))

@@ -21,9 +21,8 @@ GROUP = 512
 GROUPS = U // GROUP
 WORD_STORES = ((0, 768), (768, 1536), (1536, 2048))
 LAP = 16
-VECTOR_LOW = 592
-GPSIMD_FIRST = 720
-GPSIMD_LOW = 1792
+VECTOR_LOW = 832
+GPSIMD_LOW = 1856
 SCALAR_HIGH = 192
 LAST_PLANE = ((SCALAR_HIGH, 512), (512, 1024), (1024, 2048))
 VECTOR_WEAVES = ((512, 1024),)
@@ -124,10 +123,10 @@ def tile_picked_phput_none_po_kernel(tc, x_words, x_scales, mem, w1, offs, slot,
                 elif t == 0:
                     nc.vector.tensor_copy(halves[t][1], acc[:])
                 elif t == 2:
-                    nc.vector.tensor_copy(y2, acc[:])
+                    nc.scalar.copy(y2, acc[:])
                 else:
-                    nc.vector.tensor_copy(halves[t][0], acc[:, 0:HALF])
-                    nc.vector.tensor_copy(halves[t][1], acc[:, HALF:S])
+                    nc.scalar.copy(halves[t][0], acc[:, 0:HALF])
+                    nc.scalar.copy(halves[t][1], acc[:, HALF:S])
 
         grouped = keep.tile([P, PACK * U], BF16, name="grouped", align_bytes=64)
 
@@ -140,16 +139,14 @@ def tile_picked_phput_none_po_kernel(tc, x_words, x_scales, mem, w1, offs, slot,
 
         slot_halves = (slot_sb[:, 0 : HALF // 16], slot_sb[:, HALF // 16 : S // 16])
 
-        nc.scalar.activation(windows[0][:].indirect(slot_halves[0]), halves[0][0], copy)
-        nc.vector.tensor_copy(windows[0][:].indirect(slot_halves[1]), halves[0][1])
+        nc.vector.tensor_copy(windows[0][:].indirect(slot_sb[:]), y0[:])
         nc.sync.dma_start(out_rows[0], windows[0][:])
         nc.vector.tensor_copy(place(0, LAP, VECTOR_LOW), windows[0][:, LAP:VECTOR_LOW])
-        for lo, hi in ((VECTOR_LOW, GPSIMD_FIRST), (GPSIMD_FIRST, GPSIMD_LOW)):
-            nc.gpsimd.tensor_scalar(place(0, lo, hi), windows[0][:, lo:hi], 1.0, -0.0, mult, add)
 
         for part in range(2):
             nc.scalar.activation(windows[1][:].indirect(slot_halves[part]), halves[1][part], copy)
         nc.sync.dma_start(out_rows[1], windows[1][:])
+        nc.gpsimd.tensor_scalar(place(0, VECTOR_LOW, GPSIMD_LOW), windows[0][:, VECTOR_LOW:GPSIMD_LOW], 1.0, -0.0, mult, add)
         nc.gpsimd.tensor_scalar(place(1, VECTOR_LOW, GPSIMD_LOW), windows[1][:, VECTOR_LOW:GPSIMD_LOW], 1.0, -0.0, mult, add)
         for t in range(2):
             nc.scalar.copy(place(t, GPSIMD_LOW, U), windows[t][:, GPSIMD_LOW:U])

@@ -14,19 +14,22 @@ U8 = mybir.dt.uint8
 FP8X4 = mybir.dt.float8_e4m3fn_x4
 
 P = 128
+QUADRANT = 32
+LIST_ROWS = 16
 PACK = 4
 HALF = S // 2
 PIECE = 256
 GROUP = 512
 GROUPS = U // GROUP
-WORD_STORES = ((0, 768), (768, 1536), (1536, 2048))
+
+VECTOR_LOW_END = 832
+GPSIMD_LOW_END = 1856
 LAP = 16
-VECTOR_LOW = 832
-GPSIMD_LOW = 1856
-SCALAR_HIGH = 192
-LAST_PLANE = ((SCALAR_HIGH, 512), (512, 1024), (1024, 2048))
-VECTOR_WEAVES = ((512, 1024),)
+SCALAR_HIGH_END = 192
+VECTOR_LAST_PLANE = ((SCALAR_HIGH_END, 512), (512, 1024), (1024, 2048))
+VECTOR_WEAVE = (512, 1024)
 SCALAR_WEAVES = ((0, 512), (1024, 1536), (1536, 1792), (1792, 2048))
+WORD_STORES = ((0, 768), (768, 1536), (1536, 2048))
 
 
 def tile_picked_phput_none_po_kernel(tc, x_words, x_scales, mem, w1, offs, slot, out_0, out_1, out_2):
@@ -38,8 +41,8 @@ def tile_picked_phput_none_po_kernel(tc, x_words, x_scales, mem, w1, offs, slot,
         keep = ctx.enter_context(tc.tile_pool(name="keep", bufs=1))
         psum = ctx.enter_context(tc.psum_pool(name="psum", bufs=1))
 
-        offs_sb = lists.tile([P, S // 16], U16, name="offs_sb")
-        slot_sb = lists.tile([P, S // 16], U16, name="slot_sb")
+        offs_sb = lists.tile([P, S // LIST_ROWS], U16, name="offs_sb")
+        slot_sb = lists.tile([P, S // LIST_ROWS], U16, name="slot_sb")
         scale_table = keep.tile([P, T], U8, name="scale_table", tag="room0", align_bytes=64)
         x_scale = keep.tile([P, S], U8, name="x_scale", align_bytes=64)
         nc.vector.memset(scale_table[:].bitcast(I32), 0)
@@ -52,7 +55,7 @@ def tile_picked_phput_none_po_kernel(tc, x_words, x_scales, mem, w1, offs, slot,
         nc.sync.dma_start(offs_sb[:], offs)
         scale_rows = x_scales[0].bitcast(I32).rearrange("(g v) c -> v g c", v=2)
         for v in range(2):
-            nc.sync.dma_start(scale_table[v:P:16, :].bitcast(I32), scale_rows[v])
+            nc.sync.dma_start(scale_table[v:P:LIST_ROWS, :].bitcast(I32), scale_rows[v])
         nc.sync.dma_start(w_raw[:, 1:PACK, :], w_rows[:, 1:PACK, :])
         nc.sync.dma_start(word_table[:].bitcast(I32), word_rows)
         nc.sync.dma_start(slot_sb[:], slot)
@@ -64,7 +67,7 @@ def tile_picked_phput_none_po_kernel(tc, x_words, x_scales, mem, w1, offs, slot,
         nc.vector.tensor_copy(picked_scale[:], scale_table[:].indirect(offs_sb[:]))
         nc.vector.tensor_copy(x_scale[:].bitcast(I32), picked_scale[:].bitcast(I32))
         for v in range(2):
-            nc.sync.dma_start(x_scale[2 + v : P : 32, :].bitcast(I32), picked_scale[16 + v : P : 32, :].bitcast(I32))
+            nc.sync.dma_start(x_scale[2 + v : P : QUADRANT, :].bitcast(I32), picked_scale[LIST_ROWS + v : P : QUADRANT, :].bitcast(I32))
 
         w_scale = keep.tile([P, N], U8, name="w_scale", align_bytes=64)
         w_by_plane = w_raw[:].rearrange("p j (m h e) -> p h m e j", h=2, e=2)
@@ -77,15 +80,14 @@ def tile_picked_phput_none_po_kernel(tc, x_words, x_scales, mem, w1, offs, slot,
         nc.vector.quantize_mx(out=w_codes0[:].bitcast(FP8X4), scales=w_scale[:, 0 : 2 * P], in_=w_bf0[:])
         x_codes = keep.tile([P, S], U32, name="x_codes", align_bytes=64)
         for lo in (0, HALF):
-            nc.vector.tensor_copy(x_codes[:, lo : lo + HALF], word_table[:].indirect(offs_sb[:, lo // 16 : (lo + HALF) // 16]))
+            nc.vector.tensor_copy(x_codes[:, lo : lo + HALF], word_table[:].indirect(offs_sb[:, lo // LIST_ROWS : (lo + HALF) // LIST_ROWS]))
         w_codes1 = keep.tile([P, 2 * P], U32, name="w_codes1", align_bytes=64)
         nc.vector.quantize_mx(out=w_codes1[:].bitcast(FP8X4), scales=w_scale[:, 2 * P : N], in_=w_bf1[:])
         w_codes = (w_codes0, w_codes1)
 
-        order = (0, 1, 2, 3)
-        windows = {}
-        for room, t in enumerate(order):
-            windows[t] = keep.tile([P, U], F32, name="window%d" % t, tag="room%d" % room, align_bytes=64)
+        windows = []
+        for t in range(PACK):
+            windows.append(keep.tile([P, U], F32, name="window%d" % t, tag="room%d" % t, align_bytes=64))
             nc.sync.dma_start(windows[t][:], mem_rows[t])
 
         front = S - LAP
@@ -99,34 +101,29 @@ def tile_picked_phput_none_po_kernel(tc, x_words, x_scales, mem, w1, offs, slot,
         y1_end = keep.tile([P, HALF], F32, name="y1_end")
         y2 = pairs_and_y[:, 0 : 2 * S].bitcast(F32)
         y3_end = keep.tile([P, HALF], F32, name="y3_end")
-        halves = (
-            (y0[:, 0:HALF], y0[:, HALF:S]),
-            (pairs[:, 2 * U - S : 2 * U].bitcast(F32), y1_end[:]),
-            (y2[:, 0:HALF], y2[:, HALF:S]),
-            (pairs[:, 2 * U : 2 * U + S].bitcast(F32), y3_end[:]),
-        )
-        for t in range(PACK):
-            e, h = t % 2, t // 2
-            for lo, hi in ((0, HALF), (HALF, S)) if t == 0 else ((0, S),):
-                acc = psum.tile([P, hi - lo], F32, name="acc%d_%d" % (t, lo))
-                nc.tensor.matmul_mx(
-                    out=acc[:],
-                    lhsT=w_codes[h][:, e * P : (e + 1) * P].bitcast(FP8X4),
-                    lhsT_scale=w_scale[:, t * P : (t + 1) * P],
-                    rhs=x_codes[:, lo:hi].bitcast(FP8X4),
-                    rhs_scale=x_scale[:, lo:hi],
-                    start=True,
-                    stop=True,
-                )
-                if (t, lo) == (0, 0):
-                    nc.scalar.copy(halves[t][0], acc[:])
-                elif t == 0:
-                    nc.vector.tensor_copy(halves[t][1], acc[:])
-                elif t == 2:
-                    nc.scalar.copy(y2, acc[:])
-                else:
-                    nc.scalar.copy(halves[t][0], acc[:, 0:HALF])
-                    nc.scalar.copy(halves[t][1], acc[:, HALF:S])
+        y1_halves = (pairs[:, 2 * (U - HALF) : 2 * U].bitcast(F32), y1_end[:])
+        y3_halves = (pairs[:, 2 * U : 2 * (U + HALF)].bitcast(F32), y3_end[:])
+
+        def product(t, lo, hi):
+            acc = psum.tile([P, hi - lo], F32, name="acc%d_%d" % (t, lo))
+            nc.tensor.matmul_mx(
+                out=acc[:],
+                lhsT=w_codes[t // 2][:, t % 2 * P : (t % 2 + 1) * P].bitcast(FP8X4),
+                lhsT_scale=w_scale[:, t * P : (t + 1) * P],
+                rhs=x_codes[:, lo:hi].bitcast(FP8X4),
+                rhs_scale=x_scale[:, lo:hi],
+                start=True,
+                stop=True,
+            )
+            return acc
+
+        nc.scalar.copy(y0[:, 0:HALF], product(0, 0, HALF)[:])
+        nc.scalar.copy(y0[:, HALF:S], product(0, HALF, S)[:])
+        for t, parts in ((1, y1_halves), (2, (y2,)), (3, y3_halves)):
+            bank = product(t, 0, S)
+            width = S // len(parts)
+            for part, y in enumerate(parts):
+                nc.scalar.copy(y, bank[:, part * width : (part + 1) * width])
 
         grouped = keep.tile([P, PACK * U], BF16, name="grouped", align_bytes=64)
 
@@ -137,47 +134,46 @@ def tile_picked_phput_none_po_kernel(tc, x_words, x_scales, mem, w1, offs, slot,
         codes = keep.tile([P, U], U32, name="codes", align_bytes=64)
         out_words = out_1[0].rearrange("p c r -> p (c r)").bitcast(I32)
 
-        slot_halves = (slot_sb[:, 0 : HALF // 16], slot_sb[:, HALF // 16 : S // 16])
+        slot_halves = (slot_sb[:, 0 : HALF // LIST_ROWS], slot_sb[:, HALF // LIST_ROWS : S // LIST_ROWS])
 
         nc.vector.tensor_copy(windows[0][:].indirect(slot_sb[:]), y0[:])
         nc.sync.dma_start(out_rows[0], windows[0][:])
-        nc.vector.tensor_copy(place(0, LAP, VECTOR_LOW), windows[0][:, LAP:VECTOR_LOW])
+        nc.vector.tensor_copy(place(0, LAP, VECTOR_LOW_END), windows[0][:, LAP:VECTOR_LOW_END])
 
         for part in range(2):
-            nc.scalar.activation(windows[1][:].indirect(slot_halves[part]), halves[1][part], copy)
+            nc.scalar.activation(windows[1][:].indirect(slot_halves[part]), y1_halves[part], copy)
         nc.sync.dma_start(out_rows[1], windows[1][:])
-        nc.gpsimd.tensor_scalar(place(0, VECTOR_LOW, GPSIMD_LOW), windows[0][:, VECTOR_LOW:GPSIMD_LOW], 1.0, -0.0, mult, add)
-        nc.gpsimd.tensor_scalar(place(1, VECTOR_LOW, GPSIMD_LOW), windows[1][:, VECTOR_LOW:GPSIMD_LOW], 1.0, -0.0, mult, add)
         for t in range(2):
-            nc.scalar.copy(place(t, GPSIMD_LOW, U), windows[t][:, GPSIMD_LOW:U])
+            nc.gpsimd.tensor_scalar(place(t, VECTOR_LOW_END, GPSIMD_LOW_END), windows[t][:, VECTOR_LOW_END:GPSIMD_LOW_END], 1.0, -0.0, mult, add)
+        for t in range(2):
+            nc.scalar.copy(place(t, GPSIMD_LOW_END, U), windows[t][:, GPSIMD_LOW_END:U])
 
         nc.vector.tensor_copy(windows[2][:].indirect(slot_sb[:]), y2)
         nc.sync.dma_start(out_rows[2], windows[2][:])
-        nc.vector.tensor_copy(place(1, 0, VECTOR_LOW), windows[1][:, 0:VECTOR_LOW])
+        nc.vector.tensor_copy(place(1, 0, VECTOR_LOW_END), windows[1][:, 0:VECTOR_LOW_END])
         nc.vector.tensor_copy(place(0, 0, LAP), windows[0][:, 0:LAP])
 
         for part in range(2):
-            nc.scalar.activation(windows[3][:].indirect(slot_halves[part]), halves[3][part], copy)
+            nc.scalar.activation(windows[3][:].indirect(slot_halves[part]), y3_halves[part], copy)
         nc.sync.dma_start(out_rows[3], windows[3][:])
-        nc.vector.tensor_copy(place(2, SCALAR_HIGH, U), windows[2][:, SCALAR_HIGH:U])
+        nc.vector.tensor_copy(place(2, SCALAR_HIGH_END, U), windows[2][:, SCALAR_HIGH_END:U])
         for t in (2, 3):
-            nc.scalar.copy(place(t, 0, SCALAR_HIGH), windows[t][:, 0:SCALAR_HIGH])
-        for lo, hi in LAST_PLANE:
+            nc.scalar.copy(place(t, 0, SCALAR_HIGH_END), windows[t][:, 0:SCALAR_HIGH_END])
+        for lo, hi in VECTOR_LAST_PLANE:
             nc.vector.tensor_copy(place(3, lo, hi), windows[3][:, lo:hi])
 
-        for lo, hi in VECTOR_WEAVES:
-            nc.vector.tensor_copy(*weave_views(lo, hi, I32))
+        nc.vector.tensor_copy(*weave_views(*VECTOR_WEAVE, I32))
         for lo, hi in SCALAR_WEAVES:
             nc.scalar.copy(*weave_views(lo, hi, U32))
         for first, end in WORD_STORES:
             for lo in range(first, end, PIECE):
                 nc.vector.quantize_mx(
                     out=codes[:, lo : lo + PIECE].bitcast(FP8X4),
-                    scales=out_scale[4 * (lo // GROUP) : P, lo % GROUP : lo % GROUP + PIECE],
+                    scales=out_scale[PACK * (lo // GROUP) : P, lo % GROUP : lo % GROUP + PIECE],
                     in_=grouped[:, PACK * lo : PACK * (lo + PIECE)],
                 )
             nc.sync.dma_start(out_words[:, first:end], codes[:, first:end].bitcast(I32))
 
-        scale_out = out_2[0].bitcast(I32).rearrange("(q r) (g c) -> q g r c", r=4, g=GROUPS)
-        for q in range(4):
-            nc.sync.dma_start(scale_out[q], out_scale[32 * q : 32 * q + 16, :].bitcast(I32))
+        scale_out = out_2[0].bitcast(I32).rearrange("(q r) (a c) -> q a r c", r=PACK, a=GROUPS)
+        for q in range(P // QUADRANT):
+            nc.sync.dma_start(scale_out[q], out_scale[QUADRANT * q : QUADRANT * q + PACK * GROUPS, :].bitcast(I32))

@@ -21,6 +21,7 @@ HALF = S // 2
 PIECE = 256
 GROUP = 512
 GROUPS = U // GROUP
+DMA_ALIGN = 256
 
 VECTOR_LOW_END = 832
 GPSIMD_LOW_END = 1856
@@ -41,15 +42,15 @@ def tile_picked_phput_none_po_kernel(tc, x_words, x_scales, mem, w1, offs, slot,
         keep = ctx.enter_context(tc.tile_pool(name="keep", bufs=1))
         psum = ctx.enter_context(tc.psum_pool(name="psum", bufs=1))
 
-        offs_sb = lists.tile([P, S // LIST_ROWS], U16, name="offs_sb")
-        slot_sb = lists.tile([P, S // LIST_ROWS], U16, name="slot_sb")
-        scale_table = keep.tile([P, T], U8, name="scale_table", tag="room0", align_bytes=64)
-        x_scale = keep.tile([P, S], U8, name="x_scale", align_bytes=64)
+        offs_sb = lists.tile([P, S // LIST_ROWS], U16, name="offs_sb", align_bytes=DMA_ALIGN)
+        slot_sb = lists.tile([P, S // LIST_ROWS], U16, name="slot_sb", align_bytes=DMA_ALIGN)
+        scale_table = keep.tile([P, T], U8, name="scale_table", tag="room0", align_bytes=DMA_ALIGN)
+        x_scale = keep.tile([P, S], U8, name="x_scale", align_bytes=DMA_ALIGN)
         nc.vector.memset(scale_table[:].bitcast(I32), 0)
 
-        w_raw = keep.tile([P, PACK, N], F32, name="w_raw", align_bytes=64)
+        w_raw = keep.tile([P, PACK, N], F32, name="w_raw", align_bytes=DMA_ALIGN)
         w_rows = w1.rearrange("(p j) n -> p j n", j=PACK)
-        word_table = keep.tile([P, T], U32, name="word_table", tag="room3", align_bytes=64)
+        word_table = keep.tile([P, T], U32, name="word_table", tag="room3", align_bytes=DMA_ALIGN)
         word_rows = x_words[0].rearrange("p c r -> p (c r)").bitcast(I32)
         nc.sync.dma_start(w_raw[:, 0:1, :], w_rows[:, 0:1, :])
         nc.sync.dma_start(offs_sb[:], offs)
@@ -63,7 +64,7 @@ def tile_picked_phput_none_po_kernel(tc, x_words, x_scales, mem, w1, offs, slot,
         mem_rows = mem.rearrange("(p t) c -> t p c", t=PACK)
         out_rows = out_0.rearrange("(p t) c -> t p c", t=PACK)
 
-        picked_scale = keep.tile([P, S], U8, name="picked_scale", tag="room2", align_bytes=64)
+        picked_scale = keep.tile([P, S], U8, name="picked_scale", tag="room2", align_bytes=DMA_ALIGN)
         nc.vector.tensor_copy(picked_scale[:], scale_table[:].indirect(offs_sb[:]))
         nc.vector.tensor_copy(x_scale[:].bitcast(I32), picked_scale[:].bitcast(I32))
         for v in range(2):
@@ -71,7 +72,7 @@ def tile_picked_phput_none_po_kernel(tc, x_words, x_scales, mem, w1, offs, slot,
 
         w_scale = keep.tile([P, N], U8, name="w_scale", align_bytes=64)
         w_by_plane = w_raw[:].rearrange("p j (m h e) -> p h m e j", h=2, e=2)
-        w_bf0 = keep.tile([P, 2 * N], BF16, name="w_bf0", tag="room1", align_bytes=64)
+        w_bf0 = keep.tile([P, 2 * N], BF16, name="w_bf0", tag="room1", align_bytes=DMA_ALIGN)
         w_bf1 = keep.tile([P, 2 * N], BF16, name="w_bf1", align_bytes=64)
         nc.vector.tensor_copy(w_bf0[:].rearrange("p (e m j) -> p m e j", e=2, j=PACK), w_by_plane[:, 0])
         for rows in (slice(0, 1), slice(1, PACK)):
@@ -87,7 +88,7 @@ def tile_picked_phput_none_po_kernel(tc, x_words, x_scales, mem, w1, offs, slot,
 
         windows = []
         for t in range(PACK):
-            windows.append(keep.tile([P, U], F32, name="window%d" % t, tag="room%d" % t, align_bytes=64))
+            windows.append(keep.tile([P, U], F32, name="window%d" % t, tag="room%d" % t, align_bytes=DMA_ALIGN))
             nc.sync.dma_start(windows[t][:], mem_rows[t])
 
         front = S - LAP
@@ -130,8 +131,8 @@ def tile_picked_phput_none_po_kernel(tc, x_words, x_scales, mem, w1, offs, slot,
         def weave_views(lo, hi, dtype):
             return grouped[:].bitcast(dtype).rearrange("p (c h) -> p c h", h=2)[:, lo:hi], pairs.bitcast(dtype).rearrange("p (h c) -> p c h", h=2)[:, lo:hi]
 
-        out_scale = keep.tile([P, GROUP], U8, name="out_scale", align_bytes=64)
-        codes = keep.tile([P, U], U32, name="codes", align_bytes=64)
+        out_scale = keep.tile([P, GROUP], U8, name="out_scale", align_bytes=DMA_ALIGN)
+        codes = keep.tile([P, U], U32, name="codes", align_bytes=DMA_ALIGN)
         out_words = out_1[0].rearrange("p c r -> p (c r)").bitcast(I32)
 
         slot_halves = (slot_sb[:, 0 : HALF // LIST_ROWS], slot_sb[:, HALF // LIST_ROWS : S // LIST_ROWS])

from contextlib import ExitStack

import concourse.mybir as mybir

K, T, S, N, U = 512, 2048, 512, 512, 2048
FLOPS = 2 * K * N * S

F32 = mybir.dt.float32
BF16 = mybir.dt.bfloat16
I32 = mybir.dt.int32
U32 = mybir.dt.uint32
U16 = mybir.dt.uint16
U8 = mybir.dt.uint8
FP8X4 = mybir.dt.float8_e4m3fn_x4

P = 128
QUADRANT = 32
LIST_ROWS = 16
PACK = 4
HALF = S // 2
PIECE = 256
GROUP = 512
GROUPS = U // GROUP
DMA_ALIGN = 256

VECTOR_LOW_END = 832
GPSIMD_LOW_END = 1856
LAP = 16
SCALAR_HIGH_END = 192
VECTOR_LAST_PLANE = ((SCALAR_HIGH_END, 512), (512, 1024), (1024, 2048))
VECTOR_WEAVE = (512, 1024)
SCALAR_WEAVES = ((0, 512), (1024, 1536), (1536, 1792), (1792, 2048))
WORD_STORES = ((0, 768), (768, 1536), (1536, 2048))


def tile_picked_phput_none_po_kernel(tc, x_words, x_scales, mem, w1, offs, slot, out_0, out_1, out_2):
    nc = tc.nc
    copy = mybir.ActivationFunctionType.Copy
    mult, add = mybir.AluOpType.mult, mybir.AluOpType.add
    with ExitStack() as ctx:
        lists = ctx.enter_context(tc.tile_pool(name="lists", bufs=1))
        keep = ctx.enter_context(tc.tile_pool(name="keep", bufs=1))
        psum = ctx.enter_context(tc.psum_pool(name="psum", bufs=1))

        offs_sb = lists.tile([P, S // LIST_ROWS], U16, name="offs_sb", align_bytes=DMA_ALIGN)
        slot_sb = lists.tile([P, S // LIST_ROWS], U16, name="slot_sb", align_bytes=DMA_ALIGN)
        scale_table = keep.tile([P, T], U8, name="scale_table", tag="room0", align_bytes=DMA_ALIGN)
        x_scale = keep.tile([P, S], U8, name="x_scale", align_bytes=DMA_ALIGN)
        nc.vector.memset(scale_table[:].bitcast(I32), 0)

        w_raw = keep.tile([P, PACK, N], F32, name="w_raw", align_bytes=DMA_ALIGN)
        w_rows = w1.rearrange("(p j) n -> p j n", j=PACK)
        word_table = keep.tile([P, T], U32, name="word_table", tag="room3", align_bytes=DMA_ALIGN)
        word_rows = x_words[0].rearrange("p c r -> p (c r)").bitcast(I32)
        nc.sync.dma_start(w_raw[:, 0:1, :], w_rows[:, 0:1, :])
        nc.sync.dma_start(offs_sb[:], offs)
        scale_rows = x_scales[0].bitcast(I32).rearrange("(g v) c -> v g c", v=2)
        for v in range(2):
            nc.sync.dma_start(scale_table[v:P:LIST_ROWS, :].bitcast(I32), scale_rows[v])
        nc.sync.dma_start(w_raw[:, 1:PACK, :], w_rows[:, 1:PACK, :])
        nc.sync.dma_start(word_table[:].bitcast(I32), word_rows)
        nc.sync.dma_start(slot_sb[:], slot)

        mem_rows = mem.rearrange("(p t) c -> t p c", t=PACK)
        out_rows = out_0.rearrange("(p t) c -> t p c", t=PACK)

        picked_scale = keep.tile([P, S], U8, name="picked_scale", tag="room2", align_bytes=DMA_ALIGN)
        nc.vector.tensor_copy(picked_scale[:], scale_table[:].indirect(offs_sb[:]))
        nc.vector.tensor_copy(x_scale[:].bitcast(I32), picked_scale[:].bitcast(I32))
        for v in range(2):
            nc.sync.dma_start(x_scale[2 + v : P : QUADRANT, :].bitcast(I32), picked_scale[LIST_ROWS + v : P : QUADRANT, :].bitcast(I32))

        w_scale = keep.tile([P, N], U8, name="w_scale", align_bytes=64)
        w_by_plane = w_raw[:].rearrange("p j (m h e) -> p h m e j", h=2, e=2)
        w_bf0 = keep.tile([P, 2 * N], BF16, name="w_bf0", tag="room1", align_bytes=DMA_ALIGN)
        w_bf1 = keep.tile([P, 2 * N], BF16, name="w_bf1", align_bytes=64)
        nc.vector.tensor_copy(w_bf0[:].rearrange("p (e m j) -> p m e j", e=2, j=PACK), w_by_plane[:, 0])
        for rows in (slice(0, 1), slice(1, PACK)):
            nc.scalar.activation(w_bf1[:].rearrange("p (e m j) -> p m e j", e=2, j=PACK)[:, :, :, rows], w_by_plane[:, 1, :, :, rows], copy)
        w_codes0 = keep.tile([P, 2 * P], U32, name="w_codes0", align_bytes=64)
        nc.vector.quantize_mx(out=w_codes0[:].bitcast(FP8X4), scales=w_scale[:, 0 : 2 * P], in_=w_bf0[:])
        x_codes = keep.tile([P, S], U32, name="x_codes", align_bytes=64)
        for lo in (0, HALF):
            nc.vector.tensor_copy(x_codes[:, lo : lo + HALF], word_table[:].indirect(offs_sb[:, lo // LIST_ROWS : (lo + HALF) // LIST_ROWS]))
        w_codes1 = keep.tile([P, 2 * P], U32, name="w_codes1", align_bytes=64)
        nc.vector.quantize_mx(out=w_codes1[:].bitcast(FP8X4), scales=w_scale[:, 2 * P : N], in_=w_bf1[:])
        w_codes = (w_codes0, w_codes1)

        windows = []
        for t in range(PACK):
            windows.append(keep.tile([P, U], F32, name="window%d" % t, tag="room%d" % t, align_bytes=DMA_ALIGN))
            nc.sync.dma_start(windows[t][:], mem_rows[t])

        front = S - LAP
        pairs_and_y = keep.tile([P, 2 * front + PACK * U], BF16, name="pairs_and_y", align_bytes=64)
        pairs = pairs_and_y[:, 2 * front : 2 * front + PACK * U]

        def place(t, lo, hi):
            return pairs.rearrange("p (h c e) -> p h e c", h=2, e=2)[:, t // 2, t % 2, lo:hi]

        y0 = keep.tile([P, S], F32, name="y0")
        y1_end = keep.tile([P, HALF], F32, name="y1_end")
        y2 = pairs_and_y[:, 0 : 2 * S].bitcast(F32)
        y3_end = keep.tile([P, HALF], F32, name="y3_end")
        y1_halves = (pairs[:, 2 * (U - HALF) : 2 * U].bitcast(F32), y1_end[:])
        y3_halves = (pairs[:, 2 * U : 2 * (U + HALF)].bitcast(F32), y3_end[:])

        def product(t, lo, hi):
            acc = psum.tile([P, hi - lo], F32, name="acc%d_%d" % (t, lo))
            nc.tensor.matmul_mx(
                out=acc[:],
                lhsT=w_codes[t // 2][:, t % 2 * P : (t % 2 + 1) * P].bitcast(FP8X4),
                lhsT_scale=w_scale[:, t * P : (t + 1) * P],
                rhs=x_codes[:, lo:hi].bitcast(FP8X4),
                rhs_scale=x_scale[:, lo:hi],
                start=True,
                stop=True,
            )
            return acc

        nc.scalar.copy(y0[:, 0:HALF], product(0, 0, HALF)[:])
        nc.scalar.copy(y0[:, HALF:S], product(0, HALF, S)[:])
        for t, parts in ((1, y1_halves), (2, (y2,)), (3, y3_halves)):
            bank = product(t, 0, S)
            width = S // len(parts)
            for part, y in enumerate(parts):
                nc.scalar.copy(y, bank[:, part * width : (part + 1) * width])

        grouped = keep.tile([P, PACK * U], BF16, name="grouped", align_bytes=64)

        def weave_views(lo, hi, dtype):
            return grouped[:].bitcast(dtype).rearrange("p (c h) -> p c h", h=2)[:, lo:hi], pairs.bitcast(dtype).rearrange("p (h c) -> p c h", h=2)[:, lo:hi]

        out_scale = keep.tile([P, GROUP], U8, name="out_scale", align_bytes=DMA_ALIGN)
        codes = keep.tile([P, U], U32, name="codes", align_bytes=DMA_ALIGN)
        out_words = out_1[0].rearrange("p c r -> p (c r)").bitcast(I32)

        slot_halves = (slot_sb[:, 0 : HALF // LIST_ROWS], slot_sb[:, HALF // LIST_ROWS : S // LIST_ROWS])

        nc.vector.tensor_copy(windows[0][:].indirect(slot_sb[:]), y0[:])
        nc.sync.dma_start(out_rows[0], windows[0][:])
        nc.vector.tensor_copy(place(0, LAP, VECTOR_LOW_END), windows[0][:, LAP:VECTOR_LOW_END])

        for part in range(2):
            nc.scalar.activation(windows[1][:].indirect(slot_halves[part]), y1_halves[part], copy)
        nc.sync.dma_start(out_rows[1], windows[1][:])
        for t in range(2):
            nc.gpsimd.tensor_scalar(place(t, VECTOR_LOW_END, GPSIMD_LOW_END), windows[t][:, VECTOR_LOW_END:GPSIMD_LOW_END], 1.0, -0.0, mult, add)
        for t in range(2):
            nc.scalar.copy(place(t, GPSIMD_LOW_END, U), windows[t][:, GPSIMD_LOW_END:U])

        nc.vector.tensor_copy(windows[2][:].indirect(slot_sb[:]), y2)
        nc.sync.dma_start(out_rows[2], windows[2][:])
        nc.vector.tensor_copy(place(1, 0, VECTOR_LOW_END), windows[1][:, 0:VECTOR_LOW_END])
        nc.vector.tensor_copy(place(0, 0, LAP), windows[0][:, 0:LAP])

        for part in range(2):
            nc.scalar.activation(windows[3][:].indirect(slot_halves[part]), y3_halves[part], copy)
        nc.sync.dma_start(out_rows[3], windows[3][:])
        nc.vector.tensor_copy(place(2, SCALAR_HIGH_END, U), windows[2][:, SCALAR_HIGH_END:U])
        for t in (2, 3):
            nc.scalar.copy(place(t, 0, SCALAR_HIGH_END), windows[t][:, 0:SCALAR_HIGH_END])
        for lo, hi in VECTOR_LAST_PLANE:
            nc.vector.tensor_copy(place(3, lo, hi), windows[3][:, lo:hi])

        nc.vector.tensor_copy(*weave_views(*VECTOR_WEAVE, I32))
        for lo, hi in SCALAR_WEAVES:
            nc.scalar.copy(*weave_views(lo, hi, U32))
        for first, end in WORD_STORES:
            for lo in range(first, end, PIECE):
                nc.vector.quantize_mx(
                    out=codes[:, lo : lo + PIECE].bitcast(FP8X4),
                    scales=out_scale[PACK * (lo // GROUP) : P, lo % GROUP : lo % GROUP + PIECE],
                    in_=grouped[:, PACK * lo : PACK * (lo + PIECE)],
                )
            nc.sync.dma_start(out_words[:, first:end], codes[:, first:end].bitcast(I32))

        scale_out = out_2[0].bitcast(I32).rearrange("(q r) (a c) -> q a r c", r=PACK, a=GROUPS)
        for q in range(P // QUADRANT):
            nc.sync.dma_start(scale_out[q], out_scale[QUADRANT * q : QUADRANT * q + PACK * GROUPS, :].bitcast(I32))
